import numpy as np
import ml_dtypes


def mxq(x, axis, fmt="e4m3"):
    dtype, down = {"e4m3": (ml_dtypes.float8_e4m3fn, 7), "e5m2": (ml_dtypes.float8_e5m2, 14)}[fmt]
    v = np.moveaxis(np.asarray(x, np.float32).astype(ml_dtypes.bfloat16).astype(np.float64), axis, -1)
    blocks = v.reshape(v.shape[:-1] + (-1, 32))
    amax = np.abs(blocks).max(-1, keepdims=True)
    byte = np.maximum(np.where(amax > 0, np.frexp(amax)[1] - 1 + 127, 0) - down, 1)
    scale = np.exp2(byte - 127.0)
    codes = (blocks / scale).astype(np.float32).astype(dtype).astype(np.float64)
    return np.moveaxis((codes * scale).reshape(v.shape), -1, axis)


WIDE = False


def mx_kscale(k):
    if not WIDE:
        return np.ones(k)
    levels = np.array([10, -10, 5, -5, 0])
    if k % 512:
        return np.exp2(np.random.permutation(np.resize(levels, k // 32))).repeat(32)
    a = np.empty((k // 512, 16))
    for p in range(k // 512):
        a[p, :8] = np.random.permutation(np.resize(levels, 8))
        for g in range(8):
            far = levels[np.abs(levels - a[p, g]) >= 10]
            a[p, g + 8] = far[np.random.randint(len(far))]
    return np.exp2(a.ravel()).repeat(32)


def f64(x):
    return np.asarray(x).astype(np.float64)


def striped(idx):
    return np.tile(idx.reshape(-1, 16).T, (8, 1)).astype(np.uint16)


def unstriped(offs):
    return offs[:16].T.reshape(-1).astype(np.int64)


def sigmoid(v):
    return 1.0 / (1.0 + np.exp(-np.maximum(v, -700.0)))

def planes(y):
    n, m = y.shape
    v = y.astype(np.float32).astype(ml_dtypes.bfloat16).astype(np.float64).reshape(n // 32, 32, m)
    top = np.abs(v).max(1)
    byte = np.clip(np.where(top > 0, np.frexp(top)[1] - 1 + 127 - 7, 1), 1, 254)
    codes = (v * np.exp2(127.0 - byte)[:, None, :]).reshape(n, m).astype(np.float32).astype(ml_dtypes.float8_e4m3fn).view(np.uint8)
    words = codes.reshape(n // 512, 128, 4, m).transpose(0, 1, 3, 2)
    return np.ascontiguousarray(words), np.ascontiguousarray(byte.astype(np.uint8).reshape(n // 512, 16, m))


K, T, S, N, U = 512, 2048, 1024, 512, 1024


def setup_inputs():
    n = np.random.standard_normal
    s = mx_kscale(K)[:, None]
    return {
        "xT": (n((K, T)) * s).astype(np.float32),
        "w1": (n((K, N)) / np.sqrt(K) / s).astype(np.float32),
        "w2": (n((K, N)) / np.sqrt(K) / s).astype(np.float32),
        "w3": (n((K, N)) / np.sqrt(K) / s).astype(np.float32),
        "offs": striped(np.random.permutation(T)[:S]),
        "src": striped(np.random.permutation(S)[(S * np.random.uniform(0, 1, U) ** 4).astype(np.int64)]),
        "dst": striped(np.random.permutation(S)),
    }


def reference(xT, w1, w2, w3, offs, src, dst):
    xq = mxq(f64(xT)[:, unstriped(offs)], 0, "e4m3")
    y = mxq(f64(w1), 0, "e4m3").T @ xq
    e = mxq(f64(w2), 0, "e4m3").T @ xq
    h = mxq(f64(w3), 0, "e4m3").T @ xq
    out_0 = (sigmoid(y[:, unstriped(dst)] + e[:, unstriped(src)])) * h[:, unstriped(src)]
    return (out_0,) + planes(out_0)

@@ -1,0 +1,222 @@
+from contextlib import ExitStack
+
+import concourse.mybir as mybir
+
+K, T, S, N, U = 512, 2048, 1024, 512, 1024
+FLOPS = 3 * 2 * K * N * S
+
+F32 = mybir.dt.float32
+BF16 = mybir.dt.bfloat16
+I32 = mybir.dt.int32
+U32 = mybir.dt.uint32
+U16 = mybir.dt.uint16
+U8 = mybir.dt.uint8
+FP8X4 = mybir.dt.float8_e4m3fn_x4
+ADD = mybir.AluOpType.add
+MULT = mybir.AluOpType.mult
+SIGMOID = mybir.ActivationFunctionType.Sigmoid
+
+P = 128
+PACK = 4
+BANK = 512
+STRIPE = 16
+EDGE_CHUNKS = ((0, 512), (512, 768), (768, 1024))
+
+
+def tile_picked_edgeatt_sigmoid_lo_kernel(
+    tc, xT, w1, w2, w3, offs, src, dst, out_0, out_1, out_2
+):
+    nc = tc.nc
+    with ExitStack() as ctx:
+        lists = ctx.enter_context(tc.tile_pool(name="lists", bufs=1))
+        keep = ctx.enter_context(tc.tile_pool(name="keep", bufs=1))
+        ring = ctx.enter_context(tc.tile_pool(name="ring", bufs=3))
+        psum = ctx.enter_context(tc.psum_pool(name="psum", bufs=8))
+
+        offs_sb = lists.tile([P, S // STRIPE], U16, name="offs_sb")
+        src_sb = lists.tile([P, U // STRIPE], U16, name="src_sb")
+        dst_sb = lists.tile([P, U // STRIPE], U16, name="dst_sb")
+
+        def entries(list_sb, lo, hi):
+            return list_sb[:, lo // STRIPE : hi // STRIPE]
+
+        x_rows = xT.rearrange("(p j) c -> p j c", j=PACK)
+
+        def load_x(a, lo, hi):
+            raw = keep.tile([P, 2, hi - lo], F32, name="x_raw_%d_%d" % (a, lo))
+            nc.sync.dma_start(out=raw[:], in_=x_rows[:, 2 * a : 2 * a + 2, lo:hi])
+            return raw
+
+        def load_w(w, label, lo, hi):
+            raw = keep.tile([P, PACK, hi - lo], F32, name="w_raw_%s_%d" % (label, lo))
+            nc.sync.dma_start(out=raw[:], in_=w.rearrange("(p j) c -> p j c", j=PACK)[:, :, lo:hi])
+            return raw
+
+        xa0 = load_x(0, 0, 1024)
+        nc.sync.dma_start(offs_sb[:], offs)
+        xa1 = load_x(0, 1024, 2048)
+        xb = [load_x(1, lo, lo + 512) for lo in range(0, T, 512)]
+        w1_raw = [load_w(w1, "y", 0, 256), load_w(w1, "y", 256, 512)]
+        nc.sync.dma_start(dst_sb[:], dst)
+        w2_raw = load_w(w2, "e", 0, N)
+        nc.sync.dma_start(src_sb[:], src)
+        w3_raw = load_w(w3, "h", 0, N)
+
+        pairs = [keep.tile([P, 2 * T], BF16, name="pairs_%d" % a, align_bytes=64) for a in range(2)]
+
+        def cast_x(copy, a, raw, raw_lo, lo, hi):
+            copy(
+                out=pairs[a][:, 2 * lo : 2 * hi].rearrange("p (c i j) -> p c j i", i=4, j=2),
+                in_=raw[:, :, lo - raw_lo : hi - raw_lo].rearrange("p j (c i) -> p c j i", i=4),
+            )
+
+        x_grouped = [keep.tile([P, PACK * BANK], BF16, name="x_grouped_%d" % h, align_bytes=64) for h in range(2)]
+        x_codes = [keep.tile([P, BANK], U32, name="x_codes_%d" % h, align_bytes=64) for h in range(2)]
+        x_scales = [keep.tile([P, BANK], U8, name="x_scales_%d" % h, align_bytes=64) for h in range(2)]
+
+        def gather_x(a, h):
+            nc.vector.tensor_copy(
+                out=x_grouped[h][:].bitcast(U32).rearrange("p (s a) -> p s a", a=2)[:, :, a],
+                in_=pairs[a][:].bitcast(U32).indirect(entries(offs_sb, h * BANK, (h + 1) * BANK)),
+            )
+
+        def quantize_x(h):
+            nc.vector.quantize_mx(out=x_codes[h][:].bitcast(FP8X4), scales=x_scales[h][:], in_=x_grouped[h][:])
+
+        w_grouped = {n: keep.tile([P, PACK * N], BF16, name="w_grouped_" + n, align_bytes=64) for n in "yeh"}
+        w_codes = {n: keep.tile([P, N], U32, name="w_codes_" + n, align_bytes=64) for n in "yeh"}
+        w_scales = {n: keep.tile([P, N], U8, name="w_scales_" + n, align_bytes=64) for n in "yeh"}
+
+        def cast_w(n, raw, lo, hi):
+            nc.scalar.copy(
+                out=w_grouped[n][:].rearrange("p (t m j) -> p m j t", t=PACK, j=PACK)[:, lo // PACK : hi // PACK],
+                in_=raw[:].rearrange("p j (m t) -> p m j t", t=PACK),
+            )
+
+        def quantize_w(n, lo, hi):
+            nc.vector.quantize_mx(
+                out=w_codes[n][:, lo:hi].bitcast(FP8X4),
+                scales=w_scales[n][:, lo:hi],
+                in_=w_grouped[n][:, PACK * lo : PACK * hi],
+            )
+
+        results = {(n, t): keep.tile([P, S], F32, name="result_%s_%d" % (n, t)) for n in "yeh" for t in range(PACK)}
+
+        def product(n, t):
+            cols = slice(t * P, (t + 1) * P)
+            for h in range(2):
+                acc = psum.tile([P, BANK], F32, name="acc")
+                nc.tensor.matmul_mx(
+                    out=acc[:],
+                    lhsT=w_codes[n][:, cols].bitcast(FP8X4),
+                    lhsT_scale=w_scales[n][:, cols],
+                    rhs=x_codes[h][:].bitcast(FP8X4),
+                    rhs_scale=x_scales[h][:],
+                    start=True,
+                    stop=True,
+                )
+                nc.scalar.copy(out=results[n, t][:, h * BANK : (h + 1) * BANK], in_=acc[:])
+
+        cast_x(nc.vector.tensor_copy, 0, xa0, 0, 0, 1024)
+        cast_x(nc.vector.tensor_copy, 0, xa1, 1024, 1024, 1728)
+        cast_x(nc.scalar.copy, 0, xa1, 1024, 1728, 2048)
+        gather_x(0, 0)
+        gather_x(0, 1)
+        for q in range(3):
+            cast_x(nc.scalar.copy, 1, xb[q], 512 * q, 512 * q, 512 * (q + 1))
+        cast_x(nc.vector.tensor_copy, 1, xb[3], 1536, 1536, 2048)
+        cast_w("y", w1_raw[0], 0, 256)
+        cast_w("y", w1_raw[1], 256, 512)
+        gather_x(1, 0)
+        gather_x(1, 1)
+        quantize_x(0)
+        quantize_w("y", 0, 128)
+        quantize_x(1)
+        quantize_w("y", 128, 256)
+        quantize_w("y", 256, 512)
+
+        gate = [keep.tile([P, U], F32, name="gate_%d" % t) for t in range(PACK)]
+
+        def gather_y(t):
+            for lo in (0, BANK):
+                nc.vector.tensor_copy(
+                    out=gate[t][:, lo : lo + BANK],
+                    in_=results["y", t][:].indirect(entries(dst_sb, lo, lo + BANK)),
+                )
+
+        def gather_e(t):
+            for lo in (0, BANK):
+                both = ring.tile([P, BANK], F32, name="both")
+                nc.vector.tensor_tensor(
+                    out=both[:],
+                    in0=results["e", t][:].indirect(entries(src_sb, lo, lo + BANK)),
+                    in1=gate[t][:, lo : lo + BANK],
+                    op=ADD,
+                )
+                nc.scalar.activation(out=gate[t][:, lo : lo + BANK], in_=both[:], func=SIGMOID)
+
+        product("y", 0)
+        product("y", 1)
+        cast_w("e", w2_raw, 0, N)
+        gather_y(0)
+        product("y", 2)
+        product("y", 3)
+        quantize_w("e", 0, N)
+        gather_y(1)
+        cast_w("h", w3_raw, 0, N)
+        product("e", 0)
+        product("e", 1)
+        gather_y(2)
+        quantize_w("h", 0, N)
+        gather_y(3)
+        product("e", 2)
+        product("e", 3)
+        for t in range(PACK):
+            product("h", t)
+            gather_e(t)
+
+        out_words = keep.tile([P, U], U32, name="out_words", align_bytes=64)
+        out_scales = keep.tile([P, U], U8, name="out_scales", align_bytes=64)
+        out_rows = out_0.rearrange("(p t) c -> p t c", t=PACK)
+        words_hbm = out_1[0].rearrange("p c r -> p (c r)").bitcast(I32)
+        scales_hbm = out_2[0].bitcast(I32)
+
+        def gather_h(lo, hi):
+            message = keep.tile([P, PACK, hi - lo], F32, name="message_%d" % lo)
+            for t in range(PACK):
+                nc.vector.tensor_tensor(
+                    out=message[:, t, :],
+                    in0=results["h", t][:].indirect(entries(src_sb, lo, hi)),
+                    in1=gate[t][:, lo:hi],
+                    op=MULT,
+                )
+            nc.sync.dma_start(out=out_rows[:, :, lo:hi], in_=message[:])
+            return message
+
+        def group_out(copy, message, lo, hi):
+            grouped = keep.tile([P, PACK * (hi - lo)], BF16, name="out_grouped_%d" % lo, align_bytes=64)
+            copy(
+                out=grouped[:].rearrange("p (c i t) -> p c t i", i=4, t=PACK),
+                in_=message[:].rearrange("p t (c i) -> p c t i", i=4),
+            )
+            return grouped
+
+        def quantize_out(grouped, lo, hi):
+            nc.vector.quantize_mx(
+                out=out_words[:, lo:hi].bitcast(FP8X4), scales=out_scales[:, lo:hi], in_=grouped[:]
+            )
+            nc.sync.dma_start(out=words_hbm[:, lo:hi], in_=out_words[:, lo:hi].bitcast(I32))
+
+        (a0, a1), (b0, b1), (c0, c1) = EDGE_CHUNKS
+        ga = group_out(nc.scalar.copy, gather_h(a0, a1), a0, a1)
+        gb = group_out(nc.scalar.copy, gather_h(b0, b1), b0, b1)
+        mc = gather_h(c0, c1)
+        quantize_out(ga, a0, a1)
+        gc = group_out(nc.vector.tensor_copy, mc, c0, c1)
+        quantize_out(gb, b0, b1)
+        quantize_out(gc, c0, c1)
+        for q in range(4):
+            queue = nc.sync if q % 2 == 0 else nc.scalar
+            queue.dma_start(
+                out=scales_hbm[4 * q : 4 * q + 4, :], in_=out_scales[32 * q : 32 * q + 4, :].bitcast(I32)
+            )

@@ -20,7 +20,7 @@ P = 128
 PACK = 4
 BANK = 512
 STRIPE = 16
-EDGE_CHUNKS = ((0, 512), (512, 768), (768, 1024))
+EDGE_CHUNKS = ((0, 512), (512, 768), (768, 896), (896, 1024))
 
 
 def tile_picked_edgeatt_sigmoid_lo_kernel(
@@ -30,7 +30,6 @@ def tile_picked_edgeatt_sigmoid_lo_kernel(
     with ExitStack() as ctx:
         lists = ctx.enter_context(tc.tile_pool(name="lists", bufs=1))
         keep = ctx.enter_context(tc.tile_pool(name="keep", bufs=1))
-        ring = ctx.enter_context(tc.tile_pool(name="ring", bufs=3))
         psum = ctx.enter_context(tc.psum_pool(name="psum", bufs=8))
 
         offs_sb = lists.tile([P, S // STRIPE], U16, name="offs_sb")
@@ -56,7 +55,7 @@ def tile_picked_edgeatt_sigmoid_lo_kernel(
         nc.sync.dma_start(offs_sb[:], offs)
         xa1 = load_x(0, 1024, 2048)
         xb = [load_x(1, lo, lo + 512) for lo in range(0, T, 512)]
-        w1_raw = [load_w(w1, "y", 0, 256), load_w(w1, "y", 256, 512)]
+        w1_raw = load_w(w1, "y", 0, N)
         nc.sync.dma_start(dst_sb[:], dst)
         w2_raw = load_w(w2, "e", 0, N)
         nc.sync.dma_start(src_sb[:], src)
@@ -70,151 +69,157 @@ def tile_picked_edgeatt_sigmoid_lo_kernel(
                 in_=raw[:, :, lo - raw_lo : hi - raw_lo].rearrange("p j (c i) -> p c j i", i=4),
             )
 
-        x_grouped = [keep.tile([P, PACK * BANK], BF16, name="x_grouped_%d" % h, align_bytes=64) for h in range(2)]
-        x_codes = [keep.tile([P, BANK], U32, name="x_codes_%d" % h, align_bytes=64) for h in range(2)]
+        x_grouped = keep.tile([P, PACK * S], BF16, name="x_grouped", tag="x_grouped", align_bytes=64)
+        x_codes = [keep.tile([P, BANK], U32, name="x_codes_0", align_bytes=64)]
         x_scales = [keep.tile([P, BANK], U8, name="x_scales_%d" % h, align_bytes=64) for h in range(2)]
 
-        def gather_x(a, h):
+        def gather_x(a):
             nc.vector.tensor_copy(
-                out=x_grouped[h][:].bitcast(U32).rearrange("p (s a) -> p s a", a=2)[:, :, a],
-                in_=pairs[a][:].bitcast(U32).indirect(entries(offs_sb, h * BANK, (h + 1) * BANK)),
+                out=x_grouped[:].bitcast(U32).rearrange("p (s a) -> p s a", a=2)[:, :, a],
+                in_=pairs[a][:].bitcast(U32).indirect(offs_sb[:]),
             )
 
-        def quantize_x(h):
-            nc.vector.quantize_mx(out=x_codes[h][:].bitcast(FP8X4), scales=x_scales[h][:], in_=x_grouped[h][:])
-
-        w_grouped = {n: keep.tile([P, PACK * N], BF16, name="w_grouped_" + n, align_bytes=64) for n in "yeh"}
-        w_codes = {n: keep.tile([P, N], U32, name="w_codes_" + n, align_bytes=64) for n in "yeh"}
-        w_scales = {n: keep.tile([P, N], U8, name="w_scales_" + n, align_bytes=64) for n in "yeh"}
-
-        def cast_w(n, raw, lo, hi):
-            nc.scalar.copy(
-                out=w_grouped[n][:].rearrange("p (t m j) -> p m j t", t=PACK, j=PACK)[:, lo // PACK : hi // PACK],
-                in_=raw[:].rearrange("p j (m t) -> p m j t", t=PACK),
-            )
-
-        def quantize_w(n, lo, hi):
+        def quantize_x(h, lo, hi):
             nc.vector.quantize_mx(
-                out=w_codes[n][:, lo:hi].bitcast(FP8X4),
-                scales=w_scales[n][:, lo:hi],
-                in_=w_grouped[n][:, PACK * lo : PACK * hi],
+                out=x_codes[h][:, lo:hi].bitcast(FP8X4),
+                scales=x_scales[h][:, lo:hi],
+                in_=x_grouped[:, PACK * (h * BANK + lo) : PACK * (h * BANK + hi)],
             )
 
-        results = {(n, t): keep.tile([P, S], F32, name="result_%s_%d" % (n, t)) for n in "yeh" for t in range(PACK)}
+        w_codes = {}
+        w_scales = {}
 
-        def product(n, t):
-            cols = slice(t * P, (t + 1) * P)
-            for h in range(2):
-                acc = psum.tile([P, BANK], F32, name="acc")
+        def rounding_copy(out, in_):
+            nc.gpsimd.tensor_scalar(out=out, in0=in_, scalar1=1.0, scalar2=0.0, op0=MULT, op1=ADD)
+
+        def cast_w(copy, n, raw, lo, hi, tag, walk):
+            grouped = keep.tile(
+                [P, (hi - lo) * PACK * P], BF16, name="w_grouped_%s_%d" % (n, lo), tag=tag, align_bytes=64
+            )
+            dealt = raw[:].rearrange("p j (m t) -> p j m t", t=PACK)[:, :, :, lo:hi]
+            copy(
+                out=grouped[:].rearrange("p (t m j) -> " + walk, m=P, j=PACK),
+                in_=dealt.rearrange("p j m t -> " + walk),
+            )
+            return grouped
+
+        def quantize_w(n, grouped, first, lo, hi, tag):
+            codes = keep.tile([P, (hi - lo) * P], U32, name="w_codes_%s_%d" % (n, lo), tag=tag, align_bytes=64)
+            scales = keep.tile([P, (hi - lo) * P], U8, name="w_scales_%s_%d" % (n, lo), align_bytes=64)
+            nc.vector.quantize_mx(
+                out=codes[:].bitcast(FP8X4),
+                scales=scales[:],
+                in_=grouped[:, PACK * P * (lo - first) : PACK * P * (hi - first)],
+            )
+            for t in range(lo, hi):
+                w_codes[n, t] = codes[:, (t - lo) * P : (t - lo + 1) * P]
+                w_scales[n, t] = scales[:, (t - lo) * P : (t - lo + 1) * P]
+
+        widths = {"y": S + 352, "e": S + 16, "h": S}
+        results = {
+            (n, t): keep.tile([P, widths[n]], F32, name="result_%s_%d" % (n, t)) for n in "yeh" for t in range(PACK)
+        }
+        for n in "ye":
+            for t in range(PACK):
+                nc.gpsimd.memset(results[n, t][:, S:], 0.0)
+
+        def product(n, t, pieces=((0, 0, BANK), (1, 0, BANK))):
+            for h, lo, hi in pieces:
+                acc = psum.tile([P, hi - lo], F32, name="acc")
                 nc.tensor.matmul_mx(
                     out=acc[:],
-                    lhsT=w_codes[n][:, cols].bitcast(FP8X4),
-                    lhsT_scale=w_scales[n][:, cols],
-                    rhs=x_codes[h][:].bitcast(FP8X4),
-                    rhs_scale=x_scales[h][:],
+                    lhsT=w_codes[n, t].bitcast(FP8X4),
+                    lhsT_scale=w_scales[n, t],
+                    rhs=x_codes[h][:, lo:hi].bitcast(FP8X4),
+                    rhs_scale=x_scales[h][:, lo:hi],
                     start=True,
                     stop=True,
                 )
-                nc.scalar.copy(out=results[n, t][:, h * BANK : (h + 1) * BANK], in_=acc[:])
+                nc.scalar.copy(out=results[n, t][:, h * BANK + lo : h * BANK + hi], in_=acc[:])
 
         cast_x(nc.vector.tensor_copy, 0, xa0, 0, 0, 1024)
         cast_x(nc.vector.tensor_copy, 0, xa1, 1024, 1024, 1728)
         cast_x(nc.scalar.copy, 0, xa1, 1024, 1728, 2048)
-        gather_x(0, 0)
-        gather_x(0, 1)
+        gather_x(0)
         for q in range(3):
             cast_x(nc.scalar.copy, 1, xb[q], 512 * q, 512 * q, 512 * (q + 1))
         cast_x(nc.vector.tensor_copy, 1, xb[3], 1536, 1536, 2048)
-        cast_w("y", w1_raw[0], 0, 256)
-        cast_w("y", w1_raw[1], 256, 512)
-        gather_x(1, 0)
-        gather_x(1, 1)
-        quantize_x(0)
-        quantize_w("y", 0, 128)
-        quantize_x(1)
-        quantize_w("y", 128, 256)
-        quantize_w("y", 256, 512)
+        gather_x(1)
+        w1_first = cast_w(nc.scalar.copy, "y", w1_raw, 0, 1, "w1_first", "p m j t")
+        w1_second = cast_w(nc.scalar.copy, "y", w1_raw, 1, 2, "w1_second", "p m j t")
+        w1_high = cast_w(nc.scalar.copy, "y", w1_raw, 2, 4, "w1_high", "p m j t")
+        quantize_x(0, 0, BANK)
+        quantize_w("y", w1_first, 0, 0, 1, "codes_y0")
+        x_codes.append(keep.tile([P, BANK], U32, name="x_codes_1", tag="w1_first", align_bytes=64))
+        quantize_x(1, 0, 256)
+        quantize_x(1, 256, BANK)
+        quantize_w("y", w1_second, 1, 1, 2, "x_grouped")
+        quantize_w("y", w1_high, 2, 2, 4, "shared_h")
 
         gate = [keep.tile([P, U], F32, name="gate_%d" % t) for t in range(PACK)]
 
         def gather_y(t):
-            for lo in (0, BANK):
-                nc.vector.tensor_copy(
-                    out=gate[t][:, lo : lo + BANK],
-                    in_=results["y", t][:].indirect(entries(dst_sb, lo, lo + BANK)),
-                )
+            nc.vector.tensor_copy(out=gate[t][:], in_=results["y", t][:].indirect(dst_sb[:]))
 
         def gather_e(t):
-            for lo in (0, BANK):
-                both = ring.tile([P, BANK], F32, name="both")
-                nc.vector.tensor_tensor(
-                    out=both[:],
-                    in0=results["e", t][:].indirect(entries(src_sb, lo, lo + BANK)),
-                    in1=gate[t][:, lo : lo + BANK],
-                    op=ADD,
-                )
-                nc.scalar.activation(out=gate[t][:, lo : lo + BANK], in_=both[:], func=SIGMOID)
+            both = keep.tile([P, U], F32, name="both_%d" % t, tag="both_%d" % t)
+            nc.vector.tensor_tensor(out=both[:], in0=results["e", t][:].indirect(src_sb[:]), in1=gate[t][:], op=ADD)
+            nc.scalar.activation(out=gate[t][:], in_=both[:], func=SIGMOID)
 
-        product("y", 0)
-        product("y", 1)
-        cast_w("e", w2_raw, 0, N)
+        product("y", 0, ((0, 0, BANK), (1, 0, 256), (1, 256, BANK)))
+        w2_grouped = cast_w(rounding_copy, "e", w2_raw, 0, PACK, "w1_high", "p t m j")
+        for t in range(1, PACK):
+            product("y", t)
+        w3_grouped = cast_w(nc.scalar.copy, "h", w3_raw, 0, PACK, "shared_h", "p m j t")
         gather_y(0)
-        product("y", 2)
-        product("y", 3)
-        quantize_w("e", 0, N)
         gather_y(1)
-        cast_w("h", w3_raw, 0, N)
-        product("e", 0)
-        product("e", 1)
         gather_y(2)
-        quantize_w("h", 0, N)
+        quantize_w("e", w2_grouped, 0, 0, PACK, "codes_e")
         gather_y(3)
-        product("e", 2)
-        product("e", 3)
+        quantize_w("h", w3_grouped, 0, 0, PACK, "codes_h")
+        for n in "eh":
+            for t in range(PACK):
+                product(n, t)
         for t in range(PACK):
-            product("h", t)
             gather_e(t)
 
         out_words = keep.tile([P, U], U32, name="out_words", align_bytes=64)
         out_scales = keep.tile([P, U], U8, name="out_scales", align_bytes=64)
+        out_grouped = keep.tile([P, PACK * U], BF16, name="out_grouped", align_bytes=64)
         out_rows = out_0.rearrange("(p t) c -> p t c", t=PACK)
         words_hbm = out_1[0].rearrange("p c r -> p (c r)").bitcast(I32)
         scales_hbm = out_2[0].bitcast(I32)
 
-        def gather_h(lo, hi):
-            message = keep.tile([P, PACK, hi - lo], F32, name="message_%d" % lo)
+        def send_messages(message, first, lo, hi):
+            part = message[:, :, lo - first : hi - first]
             for t in range(PACK):
                 nc.vector.tensor_tensor(
-                    out=message[:, t, :],
+                    out=part[:, t, :],
                     in0=results["h", t][:].indirect(entries(src_sb, lo, hi)),
                     in1=gate[t][:, lo:hi],
                     op=MULT,
                 )
-            nc.sync.dma_start(out=out_rows[:, :, lo:hi], in_=message[:])
-            return message
-
-        def group_out(copy, message, lo, hi):
-            grouped = keep.tile([P, PACK * (hi - lo)], BF16, name="out_grouped_%d" % lo, align_bytes=64)
-            copy(
-                out=grouped[:].rearrange("p (c i t) -> p c t i", i=4, t=PACK),
-                in_=message[:].rearrange("p t (c i) -> p c t i", i=4),
+            nc.sync.dma_start(out=out_rows[:, :, lo:hi], in_=part)
+            nc.scalar.copy(
+                out=out_grouped[:, PACK * lo : PACK * hi].rearrange("p (c i t) -> p c t i", i=4, t=PACK),
+                in_=part.rearrange("p t (c i) -> p c t i", i=4),
             )
-            return grouped
 
         def quantize_out(grouped, lo, hi):
             nc.vector.quantize_mx(
-                out=out_words[:, lo:hi].bitcast(FP8X4), scales=out_scales[:, lo:hi], in_=grouped[:]
+                out=out_words[:, lo:hi].bitcast(FP8X4),
+                scales=out_scales[:, lo:hi],
+                in_=grouped[:, PACK * lo : PACK * hi],
             )
             nc.sync.dma_start(out=words_hbm[:, lo:hi], in_=out_words[:, lo:hi].bitcast(I32))
 
-        (a0, a1), (b0, b1), (c0, c1) = EDGE_CHUNKS
-        ga = group_out(nc.scalar.copy, gather_h(a0, a1), a0, a1)
-        gb = group_out(nc.scalar.copy, gather_h(b0, b1), b0, b1)
-        mc = gather_h(c0, c1)
-        quantize_out(ga, a0, a1)
-        gc = group_out(nc.vector.tensor_copy, mc, c0, c1)
-        quantize_out(gb, b0, b1)
-        quantize_out(gc, c0, c1)
+        early = keep.tile([P, PACK, 512], F32, name="early")
+        late = keep.tile([P, PACK, 512], F32, name="late", tag="both_3")
+        send_messages(early, 0, 0, 512)
+        for lo, hi in EDGE_CHUNKS[1:]:
+            send_messages(late, 512, lo, hi)
+        for lo, hi in ((0, 512), (512, 768), (768, 1024)):
+            quantize_out(out_grouped, lo, hi)
         for q in range(4):
             queue = nc.sync if q % 2 == 0 else nc.scalar
             queue.dma_start(

@@ -20,7 +20,6 @@ P = 128
 PACK = 4
 BANK = 512
 STRIPE = 16
-EDGE_CHUNKS = ((0, 512), (512, 768), (768, 896), (896, 1024))
 
 
 def tile_picked_edgeatt_sigmoid_lo_kernel(
@@ -123,6 +122,9 @@ def tile_picked_edgeatt_sigmoid_lo_kernel(
             for t in range(PACK):
                 nc.gpsimd.memset(results[n, t][:, S:], 0.0)
 
+        warm = keep.tile([P, 1], F32, name="warm")
+        nc.scalar.activation(out=warm[:], in_=results["y", 0][:, S : S + 1], func=SIGMOID)
+
         def product(n, t, pieces=((0, 0, BANK), (1, 0, BANK))):
             for h, lo, hi in pieces:
                 acc = psum.tile([P, hi - lo], F32, name="acc")
@@ -190,7 +192,7 @@ def tile_picked_edgeatt_sigmoid_lo_kernel(
         words_hbm = out_1[0].rearrange("p c r -> p (c r)").bitcast(I32)
         scales_hbm = out_2[0].bitcast(I32)
 
-        def send_messages(message, first, lo, hi):
+        def send_messages(message, first, lo, hi, tiles_a_store):
             part = message[:, :, lo - first : hi - first]
             for t in range(PACK):
                 nc.vector.tensor_tensor(
@@ -199,7 +201,9 @@ def tile_picked_edgeatt_sigmoid_lo_kernel(
                     in1=gate[t][:, lo:hi],
                     op=MULT,
                 )
-            nc.sync.dma_start(out=out_rows[:, :, lo:hi], in_=part)
+                if (t + 1) % tiles_a_store == 0:
+                    done = slice(t + 1 - tiles_a_store, t + 1)
+                    nc.sync.dma_start(out=out_rows[:, done, lo:hi], in_=part[:, done, :])
             nc.scalar.copy(
                 out=out_grouped[:, PACK * lo : PACK * hi].rearrange("p (c i t) -> p c t i", i=4, t=PACK),
                 in_=part.rearrange("p t (c i) -> p c t i", i=4),
@@ -213,11 +217,11 @@ def tile_picked_edgeatt_sigmoid_lo_kernel(
             )
             nc.sync.dma_start(out=words_hbm[:, lo:hi], in_=out_words[:, lo:hi].bitcast(I32))
 
-        early = keep.tile([P, PACK, 512], F32, name="early")
-        late = keep.tile([P, PACK, 512], F32, name="late", tag="both_3")
-        send_messages(early, 0, 0, 512)
-        for lo, hi in EDGE_CHUNKS[1:]:
-            send_messages(late, 512, lo, hi)
+        early = keep.tile([P, PACK, 640], F32, name="early")
+        late = keep.tile([P, PACK, 384], F32, name="late", tag="both_3")
+        send_messages(early, 0, 0, 640, 1)
+        send_messages(late, 640, 640, 896, 2)
+        send_messages(late, 640, 896, U, PACK)
         for lo, hi in ((0, 512), (512, 768), (768, 1024)):
             quantize_out(out_grouped, lo, hi)
         for q in range(4):

@@ -53,7 +53,8 @@ def tile_picked_edgeatt_sigmoid_lo_kernel(
         xa0 = load_x(0, 0, 1024)
         nc.sync.dma_start(offs_sb[:], offs)
         xa1 = load_x(0, 1024, 2048)
-        xb = [load_x(1, lo, lo + 512) for lo in range(0, T, 512)]
+        cuts = (0, 512, 1024, 1408, 1728, T)
+        xb = [load_x(1, lo, hi) for lo, hi in zip(cuts, cuts[1:])]
         w1_raw = load_w(w1, "y", 0, N)
         nc.sync.dma_start(dst_sb[:], dst)
         w2_raw = load_w(w2, "e", 0, N)
@@ -72,10 +73,10 @@ def tile_picked_edgeatt_sigmoid_lo_kernel(
         x_codes = [keep.tile([P, BANK], U32, name="x_codes_0", align_bytes=64)]
         x_scales = [keep.tile([P, BANK], U8, name="x_scales_%d" % h, align_bytes=64) for h in range(2)]
 
-        def gather_x(a):
+        def gather_x(a, lo, hi):
             nc.vector.tensor_copy(
-                out=x_grouped[:].bitcast(U32).rearrange("p (s a) -> p s a", a=2)[:, :, a],
-                in_=pairs[a][:].bitcast(U32).indirect(offs_sb[:]),
+                out=x_grouped[:].bitcast(U32).rearrange("p (s a) -> p s a", a=2)[:, lo:hi, a],
+                in_=pairs[a][:].bitcast(U32).indirect(entries(offs_sb, lo, hi)),
             )
 
         def quantize_x(h, lo, hi):
@@ -125,8 +126,8 @@ def tile_picked_edgeatt_sigmoid_lo_kernel(
         warm = keep.tile([P, 1], F32, name="warm")
         nc.scalar.activation(out=warm[:], in_=results["y", 0][:, S : S + 1], func=SIGMOID)
 
-        def product(n, t, pieces=((0, 0, BANK), (1, 0, BANK))):
-            for h, lo, hi in pieces:
+        def product(n, t, pieces=((0, 0, BANK, nc.scalar.copy), (1, 0, BANK, nc.scalar.copy))):
+            for h, lo, hi, copy in pieces:
                 acc = psum.tile([P, hi - lo], F32, name="acc")
                 nc.tensor.matmul_mx(
                     out=acc[:],
@@ -137,25 +138,25 @@ def tile_picked_edgeatt_sigmoid_lo_kernel(
                     start=True,
                     stop=True,
                 )
-                nc.scalar.copy(out=results[n, t][:, h * BANK + lo : h * BANK + hi], in_=acc[:])
+                copy(out=results[n, t][:, h * BANK + lo : h * BANK + hi], in_=acc[:])
 
         cast_x(nc.vector.tensor_copy, 0, xa0, 0, 0, 1024)
         cast_x(nc.vector.tensor_copy, 0, xa1, 1024, 1024, 1728)
         cast_x(nc.scalar.copy, 0, xa1, 1024, 1728, 2048)
-        gather_x(0)
-        for q in range(3):
-            cast_x(nc.scalar.copy, 1, xb[q], 512 * q, 512 * q, 512 * (q + 1))
-        cast_x(nc.vector.tensor_copy, 1, xb[3], 1536, 1536, 2048)
-        gather_x(1)
-        w1_first = cast_w(nc.scalar.copy, "y", w1_raw, 0, 1, "w1_first", "p m j t")
-        w1_second = cast_w(nc.scalar.copy, "y", w1_raw, 1, 2, "w1_second", "p m j t")
+        gather_x(0, 0, S)
+        for q in range(5):
+            copy = nc.scalar.copy if q < 3 else nc.vector.tensor_copy
+            cast_x(copy, 1, xb[q], cuts[q], cuts[q], cuts[q + 1])
+        gather_x(1, 0, BANK)
+        gather_x(1, BANK, S)
+        w1_first = cast_w(nc.scalar.copy, "y", w1_raw, 0, 2, "w1_first", "p m j t")
         w1_high = cast_w(nc.scalar.copy, "y", w1_raw, 2, 4, "w1_high", "p m j t")
         quantize_x(0, 0, BANK)
-        quantize_w("y", w1_first, 0, 0, 1, "codes_y0")
+        quantize_w("y", w1_first, 0, 0, 2, "codes_y0")
         x_codes.append(keep.tile([P, BANK], U32, name="x_codes_1", tag="w1_first", align_bytes=64))
         quantize_x(1, 0, 256)
         quantize_x(1, 256, BANK)
-        quantize_w("y", w1_second, 1, 1, 2, "x_grouped")
+        product("y", 0, ((0, 0, BANK, nc.vector.tensor_copy), (1, 0, 256, nc.scalar.copy), (1, 256, BANK, nc.scalar.copy)))
         quantize_w("y", w1_high, 2, 2, 4, "shared_h")
 
         gate = [keep.tile([P, U], F32, name="gate_%d" % t) for t in range(PACK)]
@@ -168,7 +169,6 @@ def tile_picked_edgeatt_sigmoid_lo_kernel(
             nc.vector.tensor_tensor(out=both[:], in0=results["e", t][:].indirect(src_sb[:]), in1=gate[t][:], op=ADD)
             nc.scalar.activation(out=gate[t][:], in_=both[:], func=SIGMOID)
 
-        product("y", 0, ((0, 0, BANK), (1, 0, 256), (1, 256, BANK)))
         w2_grouped = cast_w(rounding_copy, "e", w2_raw, 0, PACK, "w1_high", "p t m j")
         for t in range(1, PACK):
             product("y", t)
@@ -217,11 +217,11 @@ def tile_picked_edgeatt_sigmoid_lo_kernel(
             )
             nc.sync.dma_start(out=words_hbm[:, lo:hi], in_=out_words[:, lo:hi].bitcast(I32))
 
-        early = keep.tile([P, PACK, 640], F32, name="early")
-        late = keep.tile([P, PACK, 384], F32, name="late", tag="both_3")
-        send_messages(early, 0, 0, 640, 1)
-        send_messages(late, 640, 640, 896, 2)
-        send_messages(late, 640, 896, U, PACK)
+        early = keep.tile([P, PACK, 512], F32, name="early")
+        late = keep.tile([P, PACK, 512], F32, name="late", tag="both_3")
+        send_messages(early, 0, 0, 512, 2)
+        for lo, hi in ((512, 768), (768, 896), (896, U)):
+            send_messages(late, 512, lo, hi, PACK)
         for lo, hi in ((0, 512), (512, 768), (768, 1024)):
             quantize_out(out_grouped, lo, hi)
         for q in range(4):

@@ -40,21 +40,26 @@ def tile_picked_edgeatt_sigmoid_lo_kernel(
 
         x_rows = xT.rearrange("(p j) c -> p j c", j=PACK)
 
-        def load_x(a, lo, hi):
-            raw = keep.tile([P, 2, hi - lo], F32, name="x_raw_%d_%d" % (a, lo))
-            nc.sync.dma_start(out=raw[:], in_=x_rows[:, 2 * a : 2 * a + 2, lo:hi])
-            return raw
+        pieces = {0: (0, 1280), 1: (1280, T), 2: (0, 1024), 3: (1024, T)}
+        x_raw = {key: keep.tile([P, 2, hi - lo], F32, name="x_raw_%d" % key) for key, (lo, hi) in pieces.items()}
+
+        def load_x(key, rows, lo, hi):
+            first = pieces[key][0]
+            into = x_raw[key][:, rows[0] % 2 : rows[-1] % 2 + 1, lo - first : hi - first]
+            nc.sync.dma_start(out=into, in_=x_rows[:, rows[0] : rows[-1] + 1, lo:hi])
 
         def load_w(w, label, lo, hi):
             raw = keep.tile([P, PACK, hi - lo], F32, name="w_raw_%s_%d" % (label, lo))
             nc.sync.dma_start(out=raw[:], in_=w.rearrange("(p j) c -> p j c", j=PACK)[:, :, lo:hi])
             return raw
 
-        xa0 = load_x(0, 0, 1024)
+        load_x(0, (0, 1), 0, 1280)
         nc.sync.dma_start(offs_sb[:], offs)
-        xa1 = load_x(0, 1024, 2048)
-        cuts = (0, 512, 1024, 1408, 1728, T)
-        xb = [load_x(1, lo, hi) for lo, hi in zip(cuts, cuts[1:])]
+        load_x(1, (0, 1), 1280, T)
+        load_x(2, (2, 3), 0, 1024)
+        load_x(3, (2,), 1024, T)
+        load_x(3, (3,), 1024, 1600)
+        load_x(3, (3,), 1600, T)
         w1_raw = load_w(w1, "y", 0, N)
         nc.sync.dma_start(dst_sb[:], dst)
         w2_raw = load_w(w2, "e", 0, N)
@@ -63,10 +68,11 @@ def tile_picked_edgeatt_sigmoid_lo_kernel(
 
         pairs = [keep.tile([P, 2 * T], BF16, name="pairs_%d" % a, align_bytes=64) for a in range(2)]
 
-        def cast_x(copy, a, raw, raw_lo, lo, hi):
+        def cast_x(copy, key, lo, hi):
+            a, first = key // 2, pieces[key][0]
             copy(
                 out=pairs[a][:, 2 * lo : 2 * hi].rearrange("p (c i j) -> p c j i", i=4, j=2),
-                in_=raw[:, :, lo - raw_lo : hi - raw_lo].rearrange("p j (c i) -> p c j i", i=4),
+                in_=x_raw[key][:, :, lo - first : hi - first].rearrange("p j (c i) -> p c j i", i=4),
             )
 
         x_grouped = keep.tile([P, PACK * S], BF16, name="x_grouped", tag="x_grouped", align_bytes=64)
@@ -140,13 +146,16 @@ def tile_picked_edgeatt_sigmoid_lo_kernel(
                 )
                 copy(out=results[n, t][:, h * BANK + lo : h * BANK + hi], in_=acc[:])
 
-        cast_x(nc.vector.tensor_copy, 0, xa0, 0, 0, 1024)
-        cast_x(nc.vector.tensor_copy, 0, xa1, 1024, 1024, 1728)
-        cast_x(nc.scalar.copy, 0, xa1, 1024, 1728, 2048)
+        def cast_shared(a, lo, cut, hi):
+            cast_x(nc.scalar.copy, a, lo, cut)
+            cast_x(nc.vector.tensor_copy, a, cut, hi)
+
+        cast_shared(0, 0, 416, 1280)
+        cast_shared(1, 1280, 1504, T)
         gather_x(0, 0, S)
-        for q in range(5):
-            copy = nc.scalar.copy if q < 3 else nc.vector.tensor_copy
-            cast_x(copy, 1, xb[q], cuts[q], cuts[q], cuts[q + 1])
+        cast_shared(2, 0, 640, 1024)
+        cast_shared(3, 1024, 1184, 1600)
+        cast_shared(3, 1600, 1728, T)
         gather_x(1, 0, BANK)
         gather_x(1, BANK, S)
         w1_first = cast_w(nc.scalar.copy, "y", w1_raw, 0, 2, "w1_first", "p m j t")
@@ -201,7 +210,7 @@ def tile_picked_edgeatt_sigmoid_lo_kernel(
                     in1=gate[t][:, lo:hi],
                     op=MULT,
                 )
-                if (t + 1) % tiles_a_store == 0:
+                if tiles_a_store and (t + 1) % tiles_a_store == 0:
                     done = slice(t + 1 - tiles_a_store, t + 1)
                     nc.sync.dma_start(out=out_rows[:, done, lo:hi], in_=part[:, done, :])
             nc.scalar.copy(
@@ -220,8 +229,11 @@ def tile_picked_edgeatt_sigmoid_lo_kernel(
         early = keep.tile([P, PACK, 512], F32, name="early")
         late = keep.tile([P, PACK, 512], F32, name="late", tag="both_3")
         send_messages(early, 0, 0, 512, 2)
-        for lo, hi in ((512, 768), (768, 896), (896, U)):
-            send_messages(late, 512, lo, hi, PACK)
+        send_messages(late, 512, 512, 768, PACK)
+        send_messages(late, 512, 768, 896, 0)
+        send_messages(late, 512, 896, U, 0)
+        for t in (0, 2):
+            nc.sync.dma_start(out=out_rows[:, t : t + 2, 768:], in_=late[:, t : t + 2, 256:])
         for lo, hi in ((0, 512), (512, 768), (768, 1024)):
             quantize_out(out_grouped, lo, hi)
         for q in range(4):

@@ -20,6 +20,7 @@ P = 128
 PACK = 4
 BANK = 512
 STRIPE = 16
+WOVEN = 256
 
 
 def tile_picked_edgeatt_sigmoid_lo_kernel(
@@ -40,7 +41,7 @@ def tile_picked_edgeatt_sigmoid_lo_kernel(
 
         x_rows = xT.rearrange("(p j) c -> p j c", j=PACK)
 
-        pieces = {0: (0, 1280), 1: (1280, T), 2: (0, 1024), 3: (1024, T)}
+        pieces = {0: (0, 1280), 1: (1280, T), 2: (0, 512), 3: (512, 1024), 4: (1024, 1408), 5: (1408, 1728), 6: (1728, T)}
         x_raw = {key: keep.tile([P, 2, hi - lo], F32, name="x_raw_%d" % key) for key, (lo, hi) in pieces.items()}
 
         def load_x(key, rows, lo, hi):
@@ -56,10 +57,8 @@ def tile_picked_edgeatt_sigmoid_lo_kernel(
         load_x(0, (0, 1), 0, 1280)
         nc.sync.dma_start(offs_sb[:], offs)
         load_x(1, (0, 1), 1280, T)
-        load_x(2, (2, 3), 0, 1024)
-        load_x(3, (2,), 1024, T)
-        load_x(3, (3,), 1024, 1600)
-        load_x(3, (3,), 1600, T)
+        for key in range(2, 7):
+            load_x(key, (2, 3), *pieces[key])
         w1_raw = load_w(w1, "y", 0, N)
         nc.sync.dma_start(dst_sb[:], dst)
         w2_raw = load_w(w2, "e", 0, N)
@@ -69,7 +68,7 @@ def tile_picked_edgeatt_sigmoid_lo_kernel(
         pairs = [keep.tile([P, 2 * T], BF16, name="pairs_%d" % a, align_bytes=64) for a in range(2)]
 
         def cast_x(copy, key, lo, hi):
-            a, first = key // 2, pieces[key][0]
+            a, first = min(key // 2, 1), pieces[key][0]
             copy(
                 out=pairs[a][:, 2 * lo : 2 * hi].rearrange("p (c i j) -> p c j i", i=4, j=2),
                 in_=x_raw[key][:, :, lo - first : hi - first].rearrange("p j (c i) -> p c j i", i=4),
@@ -79,11 +78,11 @@ def tile_picked_edgeatt_sigmoid_lo_kernel(
         x_codes = [keep.tile([P, BANK], U32, name="x_codes_0", align_bytes=64)]
         x_scales = [keep.tile([P, BANK], U8, name="x_scales_%d" % h, align_bytes=64) for h in range(2)]
 
-        def gather_x(a, lo, hi):
-            nc.vector.tensor_copy(
-                out=x_grouped[:].bitcast(U32).rearrange("p (s a) -> p s a", a=2)[:, lo:hi, a],
-                in_=pairs[a][:].bitcast(U32).indirect(entries(offs_sb, lo, hi)),
-            )
+        x_words = x_grouped[:].bitcast(U32).rearrange("p (s a) -> p s a", a=2)
+        x_apart = keep.tile([P, 2, WOVEN], U32, name="x_apart", align_bytes=64)
+
+        def gather_x(a, out, lo, hi):
+            nc.vector.tensor_copy(out=out, in_=pairs[a][:].bitcast(U32).indirect(entries(offs_sb, lo, hi)))
 
         def quantize_x(h, lo, hi):
             nc.vector.quantize_mx(
@@ -98,15 +97,18 @@ def tile_picked_edgeatt_sigmoid_lo_kernel(
         def rounding_copy(out, in_):
             nc.gpsimd.tensor_scalar(out=out, in0=in_, scalar1=1.0, scalar2=0.0, op0=MULT, op1=ADD)
 
+        def deal_w(copy, grouped, raw, lo, hi, walk):
+            dealt = raw[:].rearrange("p j (m t) -> p j m t", t=PACK)[:, :, :, lo:hi]
+            copy(
+                out=grouped.rearrange("p (t m j) -> " + walk, m=P, j=PACK),
+                in_=dealt.rearrange("p j m t -> " + walk),
+            )
+
         def cast_w(copy, n, raw, lo, hi, tag, walk):
             grouped = keep.tile(
                 [P, (hi - lo) * PACK * P], BF16, name="w_grouped_%s_%d" % (n, lo), tag=tag, align_bytes=64
             )
-            dealt = raw[:].rearrange("p j (m t) -> p j m t", t=PACK)[:, :, :, lo:hi]
-            copy(
-                out=grouped[:].rearrange("p (t m j) -> " + walk, m=P, j=PACK),
-                in_=dealt.rearrange("p j m t -> " + walk),
-            )
+            deal_w(copy, grouped[:], raw, lo, hi, walk)
             return grouped
 
         def quantize_w(n, grouped, first, lo, hi, tag):
@@ -132,18 +134,22 @@ def tile_picked_edgeatt_sigmoid_lo_kernel(
         warm = keep.tile([P, 1], F32, name="warm")
         nc.scalar.activation(out=warm[:], in_=results["y", 0][:, S : S + 1], func=SIGMOID)
 
+        def multiply(n, t, h, lo, hi):
+            acc = psum.tile([P, hi - lo], F32, name="acc")
+            nc.tensor.matmul_mx(
+                out=acc[:],
+                lhsT=w_codes[n, t].bitcast(FP8X4),
+                lhsT_scale=w_scales[n, t],
+                rhs=x_codes[h][:, lo:hi].bitcast(FP8X4),
+                rhs_scale=x_scales[h][:, lo:hi],
+                start=True,
+                stop=True,
+            )
+            return acc
+
         def product(n, t, pieces=((0, 0, BANK, nc.scalar.copy), (1, 0, BANK, nc.scalar.copy))):
             for h, lo, hi, copy in pieces:
-                acc = psum.tile([P, hi - lo], F32, name="acc")
-                nc.tensor.matmul_mx(
-                    out=acc[:],
-                    lhsT=w_codes[n, t].bitcast(FP8X4),
-                    lhsT_scale=w_scales[n, t],
-                    rhs=x_codes[h][:, lo:hi].bitcast(FP8X4),
-                    rhs_scale=x_scales[h][:, lo:hi],
-                    start=True,
-                    stop=True,
-                )
+                acc = multiply(n, t, h, lo, hi)
                 copy(out=results[n, t][:, h * BANK + lo : h * BANK + hi], in_=acc[:])
 
         def cast_shared(a, lo, cut, hi):
@@ -152,12 +158,14 @@ def tile_picked_edgeatt_sigmoid_lo_kernel(
 
         cast_shared(0, 0, 416, 1280)
         cast_shared(1, 1280, 1504, T)
-        gather_x(0, 0, S)
-        cast_shared(2, 0, 640, 1024)
-        cast_shared(3, 1024, 1184, 1600)
-        cast_shared(3, 1600, 1728, T)
-        gather_x(1, 0, BANK)
-        gather_x(1, BANK, S)
+        gather_x(0, x_apart[:, 0, :], 0, WOVEN)
+        gather_x(0, x_words[:, WOVEN:, 0], WOVEN, S)
+        for key in range(2, 7):
+            cast_x(nc.scalar.copy if key < 5 else nc.vector.tensor_copy, key, *pieces[key])
+        gather_x(1, x_apart[:, 1, :], 0, WOVEN)
+        nc.scalar.copy(out=x_words[:, :WOVEN, :], in_=x_apart[:].rearrange("p a s -> p s a"))
+        gather_x(1, x_words[:, WOVEN:768, 1], WOVEN, 768)
+        gather_x(1, x_words[:, 768:, 1], 768, S)
         w1_first = cast_w(nc.scalar.copy, "y", w1_raw, 0, 2, "w1_first", "p m j t")
         w1_high = cast_w(nc.scalar.copy, "y", w1_raw, 2, 4, "w1_high", "p m j t")
         quantize_x(0, 0, BANK)
@@ -178,10 +186,15 @@ def tile_picked_edgeatt_sigmoid_lo_kernel(
             nc.vector.tensor_tensor(out=both[:], in0=results["e", t][:].indirect(src_sb[:]), in1=gate[t][:], op=ADD)
             nc.scalar.activation(out=gate[t][:], in_=both[:], func=SIGMOID)
 
-        w2_grouped = cast_w(rounding_copy, "e", w2_raw, 0, PACK, "w1_high", "p t m j")
-        for t in range(1, PACK):
-            product("y", t)
-        w3_grouped = cast_w(nc.scalar.copy, "h", w3_raw, 0, PACK, "shared_h", "p m j t")
+        product("y", 1)
+        product("y", 2)
+        last_banks = [multiply("y", 3, h, 0, BANK) for h in range(2)]
+        w2_grouped = keep.tile([P, PACK * PACK * P], BF16, name="w_grouped_e", tag="shared_h", align_bytes=64)
+        deal_w(rounding_copy, w2_grouped[:, : 2 * PACK * P], w2_raw, 0, 2, "p t m j")
+        deal_w(nc.scalar.copy, w2_grouped[:, 2 * PACK * P :], w2_raw, 2, PACK, "p m j t")
+        for h in range(2):
+            nc.scalar.copy(out=results["y", 3][:, h * BANK : (h + 1) * BANK], in_=last_banks[h][:])
+        w3_grouped = cast_w(nc.scalar.copy, "h", w3_raw, 0, PACK, "w1_high", "p m j t")
         gather_y(0)
         gather_y(1)
         gather_y(2)

@@ -20,7 +20,7 @@ P = 128
 PACK = 4
 BANK = 512
 STRIPE = 16
-WOVEN = 256
+WOVEN = 512
 
 
 def tile_picked_edgeatt_sigmoid_lo_kernel(
@@ -41,7 +41,7 @@ def tile_picked_edgeatt_sigmoid_lo_kernel(
 
         x_rows = xT.rearrange("(p j) c -> p j c", j=PACK)
 
-        pieces = {0: (0, 1280), 1: (1280, T), 2: (0, 512), 3: (512, 1024), 4: (1024, 1408), 5: (1408, 1728), 6: (1728, T)}
+        pieces = {0: (0, 1280), 1: (1280, T), 2: (0, 640), 3: (640, 1280), 4: (1280, 1696), 5: (1696, T)}
         x_raw = {key: keep.tile([P, 2, hi - lo], F32, name="x_raw_%d" % key) for key, (lo, hi) in pieces.items()}
 
         def load_x(key, rows, lo, hi):
@@ -57,7 +57,7 @@ def tile_picked_edgeatt_sigmoid_lo_kernel(
         load_x(0, (0, 1), 0, 1280)
         nc.sync.dma_start(offs_sb[:], offs)
         load_x(1, (0, 1), 1280, T)
-        for key in range(2, 7):
+        for key in range(2, 6):
             load_x(key, (2, 3), *pieces[key])
         w1_raw = load_w(w1, "y", 0, N)
         nc.sync.dma_start(dst_sb[:], dst)
@@ -160,12 +160,12 @@ def tile_picked_edgeatt_sigmoid_lo_kernel(
         cast_shared(1, 1280, 1504, T)
         gather_x(0, x_apart[:, 0, :], 0, WOVEN)
         gather_x(0, x_words[:, WOVEN:, 0], WOVEN, S)
-        for key in range(2, 7):
-            cast_x(nc.scalar.copy if key < 5 else nc.vector.tensor_copy, key, *pieces[key])
-        gather_x(1, x_apart[:, 1, :], 0, WOVEN)
-        nc.scalar.copy(out=x_words[:, :WOVEN, :], in_=x_apart[:].rearrange("p a s -> p s a"))
-        gather_x(1, x_words[:, WOVEN:768, 1], WOVEN, 768)
-        gather_x(1, x_words[:, 768:, 1], 768, S)
+        for key in range(2, 6):
+            cast_x(nc.scalar.copy if key < 4 else nc.vector.tensor_copy, key, *pieces[key])
+        for lo, hi in ((0, 256), (256, WOVEN)):
+            gather_x(1, x_apart[:, 1, lo:hi], lo, hi)
+            nc.scalar.copy(out=x_words[:, lo:hi, :], in_=x_apart[:, :, lo:hi].rearrange("p a s -> p s a"))
+        gather_x(1, x_words[:, WOVEN:, 1], WOVEN, S)
         w1_first = cast_w(nc.scalar.copy, "y", w1_raw, 0, 2, "w1_first", "p m j t")
         w1_high = cast_w(nc.scalar.copy, "y", w1_raw, 2, 4, "w1_high", "p m j t")
         quantize_x(0, 0, BANK)

@@ -20,7 +20,6 @@ P = 128
 PACK = 4
 BANK = 512
 STRIPE = 16
-WOVEN = 512
 
 
 def tile_picked_edgeatt_sigmoid_lo_kernel(
@@ -41,7 +40,7 @@ def tile_picked_edgeatt_sigmoid_lo_kernel(
 
         x_rows = xT.rearrange("(p j) c -> p j c", j=PACK)
 
-        pieces = {0: (0, 1280), 1: (1280, T), 2: (0, 640), 3: (640, 1280), 4: (1280, 1696), 5: (1696, T)}
+        pieces = {0: (0, 1280), 1: (1280, T), 2: (0, 768), 3: (768, 1408), 4: (1408, 1792), 5: (1792, T)}
         x_raw = {key: keep.tile([P, 2, hi - lo], F32, name="x_raw_%d" % key) for key, (lo, hi) in pieces.items()}
 
         def load_x(key, rows, lo, hi):
@@ -74,12 +73,17 @@ def tile_picked_edgeatt_sigmoid_lo_kernel(
                 in_=x_raw[key][:, :, lo - first : hi - first].rearrange("p j (c i) -> p c j i", i=4),
             )
 
-        x_grouped = keep.tile([P, PACK * S], BF16, name="x_grouped", tag="x_grouped", align_bytes=64)
+        x_grouped = [keep.tile([P, PACK * BANK], BF16, name="x_grouped_0", align_bytes=64)]
         x_codes = [keep.tile([P, BANK], U32, name="x_codes_0", align_bytes=64)]
         x_scales = [keep.tile([P, BANK], U8, name="x_scales_%d" % h, align_bytes=64) for h in range(2)]
 
-        x_words = x_grouped[:].bitcast(U32).rearrange("p (s a) -> p s a", a=2)
-        x_apart = keep.tile([P, 2, WOVEN], U32, name="x_apart", align_bytes=64)
+        x_apart = [
+            keep.tile([P, 2, BANK], U32, name="x_apart_%d" % h, tag="x_apart_%d" % h, align_bytes=64) for h in range(2)
+        ]
+
+        def weave(copy, dtype, h, lo, hi):
+            words = x_grouped[h][:].bitcast(dtype).rearrange("p (s a) -> p s a", a=2)
+            copy(out=words[:, lo:hi, :], in_=x_apart[h][:].bitcast(dtype)[:, :, lo:hi].rearrange("p a s -> p s a"))
 
         def gather_x(a, out, lo, hi):
             nc.vector.tensor_copy(out=out, in_=pairs[a][:].bitcast(U32).indirect(entries(offs_sb, lo, hi)))
@@ -88,7 +92,7 @@ def tile_picked_edgeatt_sigmoid_lo_kernel(
             nc.vector.quantize_mx(
                 out=x_codes[h][:, lo:hi].bitcast(FP8X4),
                 scales=x_scales[h][:, lo:hi],
-                in_=x_grouped[:, PACK * (h * BANK + lo) : PACK * (h * BANK + hi)],
+                in_=x_grouped[h][:, PACK * lo : PACK * hi],
             )
 
         w_codes = {}
@@ -158,17 +162,21 @@ def tile_picked_edgeatt_sigmoid_lo_kernel(
 
         cast_shared(0, 0, 416, 1280)
         cast_shared(1, 1280, 1504, T)
-        gather_x(0, x_apart[:, 0, :], 0, WOVEN)
-        gather_x(0, x_words[:, WOVEN:, 0], WOVEN, S)
-        for key in range(2, 6):
-            cast_x(nc.scalar.copy if key < 4 else nc.vector.tensor_copy, key, *pieces[key])
-        for lo, hi in ((0, 256), (256, WOVEN)):
-            gather_x(1, x_apart[:, 1, lo:hi], lo, hi)
-            nc.scalar.copy(out=x_words[:, lo:hi, :], in_=x_apart[:, :, lo:hi].rearrange("p a s -> p s a"))
-        gather_x(1, x_words[:, WOVEN:, 1], WOVEN, S)
+        gather_x(0, x_apart[0][:, 0, :], 0, BANK)
+        gather_x(0, x_apart[1][:, 0, :], BANK, S)
+        cast_x(nc.scalar.copy, 2, *pieces[2])
+        cast_shared(3, 768, 1152, 1408)
+        cast_x(nc.vector.tensor_copy, 4, *pieces[4])
+        cast_shared(5, 1792, 1888, T)
+        for lo, hi in ((0, 256), (256, BANK)):
+            gather_x(1, x_apart[0][:, 1, lo:hi], lo, hi)
+            weave(nc.scalar.copy, U32, 0, lo, hi)
+        gather_x(1, x_apart[1][:, 1, :], BANK, S)
         w1_first = cast_w(nc.scalar.copy, "y", w1_raw, 0, 2, "w1_first", "p m j t")
         w1_high = cast_w(nc.scalar.copy, "y", w1_raw, 2, 4, "w1_high", "p m j t")
         quantize_x(0, 0, BANK)
+        x_grouped.append(keep.tile([P, PACK * BANK], BF16, name="x_grouped_1", tag="x_apart_0", align_bytes=64))
+        weave(nc.vector.tensor_copy, I32, 1, 0, BANK)
         quantize_w("y", w1_first, 0, 0, 2, "codes_y0")
         x_codes.append(keep.tile([P, BANK], U32, name="x_codes_1", tag="w1_first", align_bytes=64))
         quantize_x(1, 0, 256)
@@ -214,41 +222,61 @@ def tile_picked_edgeatt_sigmoid_lo_kernel(
         words_hbm = out_1[0].rearrange("p c r -> p (c r)").bitcast(I32)
         scales_hbm = out_2[0].bitcast(I32)
 
-        def send_messages(message, first, lo, hi, tiles_a_store):
-            part = message[:, :, lo - first : hi - first]
-            for t in range(PACK):
-                nc.vector.tensor_tensor(
-                    out=part[:, t, :],
-                    in0=results["h", t][:].indirect(entries(src_sb, lo, hi)),
-                    in1=gate[t][:, lo:hi],
-                    op=MULT,
-                )
-                if tiles_a_store and (t + 1) % tiles_a_store == 0:
-                    done = slice(t + 1 - tiles_a_store, t + 1)
-                    nc.sync.dma_start(out=out_rows[:, done, lo:hi], in_=part[:, done, :])
-            nc.scalar.copy(
-                out=out_grouped[:, PACK * lo : PACK * hi].rearrange("p (c i t) -> p c t i", i=4, t=PACK),
-                in_=part.rearrange("p t (c i) -> p c t i", i=4),
+        early = keep.tile([P, PACK, 512], F32, name="early")
+        late = keep.tile([P, PACK, 512], F32, name="late", tag="both_3")
+
+        def messages(tiles, lo, hi):
+            held, first = (early, 0) if lo < 512 else (late, 512)
+            return held[:, tiles, lo - first : hi - first]
+
+        def gather_h(t, lo, hi):
+            nc.vector.tensor_tensor(
+                out=messages(t, lo, hi),
+                in0=results["h", t][:].indirect(entries(src_sb, lo, hi)),
+                in1=gate[t][:, lo:hi],
+                op=MULT,
             )
 
-        def quantize_out(grouped, lo, hi):
+        def store_messages(t, lo, hi):
+            nc.sync.dma_start(out=out_rows[:, t : t + 2, lo:hi], in_=messages(slice(t, t + 2), lo, hi))
+
+        def interleave(lo, hi):
+            nc.scalar.copy(
+                out=out_grouped[:, PACK * lo : PACK * hi].rearrange("p (c i t) -> p c t i", i=4, t=PACK),
+                in_=messages(slice(0, PACK), lo, hi).rearrange("p t (c i) -> p c t i", i=4),
+            )
+
+        def quantize_out(lo, hi):
             nc.vector.quantize_mx(
                 out=out_words[:, lo:hi].bitcast(FP8X4),
                 scales=out_scales[:, lo:hi],
-                in_=grouped[:, PACK * lo : PACK * hi],
+                in_=out_grouped[:, PACK * lo : PACK * hi],
             )
+
+        def store_words(lo, hi):
             nc.sync.dma_start(out=words_hbm[:, lo:hi], in_=out_words[:, lo:hi].bitcast(I32))
 
-        early = keep.tile([P, PACK, 512], F32, name="early")
-        late = keep.tile([P, PACK, 512], F32, name="late", tag="both_3")
-        send_messages(early, 0, 0, 512, 2)
-        send_messages(late, 512, 512, 768, PACK)
-        send_messages(late, 512, 768, 896, 0)
-        send_messages(late, 512, 896, U, 0)
         for t in (0, 2):
-            nc.sync.dma_start(out=out_rows[:, t : t + 2, 768:], in_=late[:, t : t + 2, 256:])
-        for lo, hi in ((0, 512), (512, 768), (768, 1024)):
-            quantize_out(out_grouped, lo, hi)
+            gather_h(t, 0, 512)
+            gather_h(t + 1, 0, 512)
+            store_messages(t, 0, 512)
+        interleave(0, 512)
+        gather_h(0, 512, U)
+        gather_h(1, 512, U)
+        store_messages(0, 512, U)
+        for lo, hi in ((512, 768), (768, 896), (896, U)):
+            gather_h(2, lo, hi)
+            gather_h(3, lo, hi)
+            if hi != 896:
+                store_messages(2, hi - 256, hi)
+            interleave(lo, hi)
+        quantize_out(0, 512)
+        store_words(0, 512)
+        quantize_out(512, 768)
+        store_words(512, 768)
+        quantize_out(768, 896)
+        quantize_out(896, U)
+        store_words(768, U)
         for q in range(4):
             queue = nc.sync if q % 2 == 0 else nc.scalar
             queue.dma_start(

@@ -82,8 +82,12 @@ def tile_picked_edgeatt_sigmoid_lo_kernel(
         ]
 
         def weave(copy, dtype, h, lo, hi):
-            words = x_grouped[h][:].bitcast(dtype).rearrange("p (s a) -> p s a", a=2)
-            copy(out=words[:, lo:hi, :], in_=x_apart[h][:].bitcast(dtype)[:, :, lo:hi].rearrange("p a s -> p s a"))
+            words = x_grouped[h][:].bitcast(dtype)[:, 2 * lo : 2 * hi]
+            rows = x_apart[h][:].rearrange("p a s -> p (a s)").bitcast(dtype).rearrange("p (a s) -> p a s", a=2)
+            copy(
+                out=words.rearrange("p (c i a) -> p c a i", i=2, a=2),
+                in_=rows[:, :, lo:hi].rearrange("p a (c i) -> p c a i", i=2),
+            )
 
         def gather_x(a, out, lo, hi):
             nc.vector.tensor_copy(out=out, in_=pairs[a][:].bitcast(U32).indirect(entries(offs_sb, lo, hi)))
@@ -165,9 +169,9 @@ def tile_picked_edgeatt_sigmoid_lo_kernel(
         gather_x(0, x_apart[0][:, 0, :], 0, BANK)
         gather_x(0, x_apart[1][:, 0, :], BANK, S)
         cast_x(nc.scalar.copy, 2, *pieces[2])
-        cast_shared(3, 768, 1152, 1408)
+        cast_shared(3, 768, 1120, 1408)
         cast_x(nc.vector.tensor_copy, 4, *pieces[4])
-        cast_shared(5, 1792, 1888, T)
+        cast_shared(5, 1792, 1872, T)
         for lo, hi in ((0, 256), (256, BANK)):
             gather_x(1, x_apart[0][:, 1, lo:hi], lo, hi)
             weave(nc.scalar.copy, U32, 0, lo, hi)
@@ -261,21 +265,24 @@ def tile_picked_edgeatt_sigmoid_lo_kernel(
             gather_h(t + 1, 0, 512)
             store_messages(t, 0, 512)
         interleave(0, 512)
-        gather_h(0, 512, U)
-        gather_h(1, 512, U)
+        for t in (0, 2):
+            gather_h(t, 512, 768)
+            gather_h(t + 1, 512, 768)
+        store_messages(2, 512, 768)
+        interleave(512, 768)
+        gather_h(0, 768, U)
+        gather_h(1, 768, U)
         store_messages(0, 512, U)
-        for lo, hi in ((512, 768), (768, 896), (896, U)):
+        for lo, hi in ((768, 896), (896, U)):
             gather_h(2, lo, hi)
             gather_h(3, lo, hi)
-            if hi != 896:
-                store_messages(2, hi - 256, hi)
             interleave(lo, hi)
+        store_messages(2, 768, U)
         quantize_out(0, 512)
         store_words(0, 512)
         quantize_out(512, 768)
         store_words(512, 768)
-        quantize_out(768, 896)
-        quantize_out(896, U)
+        quantize_out(768, U)
         store_words(768, U)
         for q in range(4):
             queue = nc.sync if q % 2 == 0 else nc.scalar

@@ -14,6 +14,7 @@ U8 = mybir.dt.uint8
 FP8X4 = mybir.dt.float8_e4m3fn_x4
 ADD = mybir.AluOpType.add
 MULT = mybir.AluOpType.mult
+COPY = mybir.ActivationFunctionType.Copy
 SIGMOID = mybir.ActivationFunctionType.Sigmoid
 
 P = 128
@@ -73,17 +74,18 @@ def tile_picked_edgeatt_sigmoid_lo_kernel(
                 in_=x_raw[key][:, :, lo - first : hi - first].rearrange("p j (c i) -> p c j i", i=4),
             )
 
-        x_grouped = [keep.tile([P, PACK * BANK], BF16, name="x_grouped_0", align_bytes=64)]
-        x_codes = [keep.tile([P, BANK], U32, name="x_codes_0", align_bytes=64)]
+        x_grouped = {0: keep.tile([P, PACK * BANK], BF16, name="x_grouped_0", align_bytes=64)}
+        x_codes = {}
         x_scales = [keep.tile([P, BANK], U8, name="x_scales_%d" % h, align_bytes=64) for h in range(2)]
 
-        x_apart = [
-            keep.tile([P, 2, BANK], U32, name="x_apart_%d" % h, tag="x_apart_%d" % h, align_bytes=64) for h in range(2)
-        ]
+        x_apart = {
+            lo: keep.tile([P, 2, hi - lo], U32, name="x_apart_%d" % lo, tag="x_apart_%d" % lo, align_bytes=64)
+            for lo, hi in ((0, BANK), (BANK, 768), (768, S))
+        }
 
-        def weave(copy, dtype, h, lo, hi):
-            words = x_grouped[h][:].bitcast(dtype)[:, 2 * lo : 2 * hi]
-            rows = x_apart[h][:].rearrange("p a s -> p (a s)").bitcast(dtype).rearrange("p (a s) -> p a s", a=2)
+        def weave(copy, dtype, first, lo, hi):
+            words = x_grouped[first][:].bitcast(dtype)[:, 2 * lo : 2 * hi]
+            rows = x_apart[first][:].rearrange("p a s -> p (a s)").bitcast(dtype).rearrange("p (a s) -> p a s", a=2)
             copy(
                 out=words.rearrange("p (c i a) -> p c a i", i=2, a=2),
                 in_=rows[:, :, lo:hi].rearrange("p a (c i) -> p c a i", i=2),
@@ -93,10 +95,11 @@ def tile_picked_edgeatt_sigmoid_lo_kernel(
             nc.vector.tensor_copy(out=out, in_=pairs[a][:].bitcast(U32).indirect(entries(offs_sb, lo, hi)))
 
         def quantize_x(h, lo, hi):
+            first = h * BANK + lo
             nc.vector.quantize_mx(
                 out=x_codes[h][:, lo:hi].bitcast(FP8X4),
                 scales=x_scales[h][:, lo:hi],
-                in_=x_grouped[h][:, PACK * lo : PACK * hi],
+                in_=x_grouped[first][:],
             )
 
         w_codes = {}
@@ -105,10 +108,10 @@ def tile_picked_edgeatt_sigmoid_lo_kernel(
         def rounding_copy(out, in_):
             nc.gpsimd.tensor_scalar(out=out, in0=in_, scalar1=1.0, scalar2=0.0, op0=MULT, op1=ADD)
 
-        def deal_w(copy, grouped, raw, lo, hi, walk):
-            dealt = raw[:].rearrange("p j (m t) -> p j m t", t=PACK)[:, :, :, lo:hi]
+        def deal_w(copy, grouped, raw, lo, hi, walk, rows=slice(0, P)):
+            dealt = raw[:].rearrange("p j (m t) -> p j m t", t=PACK)[:, :, rows, lo:hi]
             copy(
-                out=grouped.rearrange("p (t m j) -> " + walk, m=P, j=PACK),
+                out=grouped.rearrange("p (t m j) -> p t m j", m=P, j=PACK)[:, :, rows, :].rearrange("p t m j -> " + walk),
                 in_=dealt.rearrange("p j m t -> " + walk),
             )
 
@@ -167,7 +170,8 @@ def tile_picked_edgeatt_sigmoid_lo_kernel(
         cast_shared(0, 0, 416, 1280)
         cast_shared(1, 1280, 1504, T)
         gather_x(0, x_apart[0][:, 0, :], 0, BANK)
-        gather_x(0, x_apart[1][:, 0, :], BANK, S)
+        gather_x(0, x_apart[BANK][:, 0, :], BANK, 768)
+        gather_x(0, x_apart[768][:, 0, :], 768, S)
         cast_x(nc.scalar.copy, 2, *pieces[2])
         cast_shared(3, 768, 1120, 1408)
         cast_x(nc.vector.tensor_copy, 4, *pieces[4])
@@ -175,17 +179,37 @@ def tile_picked_edgeatt_sigmoid_lo_kernel(
         for lo, hi in ((0, 256), (256, BANK)):
             gather_x(1, x_apart[0][:, 1, lo:hi], lo, hi)
             weave(nc.scalar.copy, U32, 0, lo, hi)
-        gather_x(1, x_apart[1][:, 1, :], BANK, S)
-        w1_first = cast_w(nc.scalar.copy, "y", w1_raw, 0, 2, "w1_first", "p m j t")
-        w1_high = cast_w(nc.scalar.copy, "y", w1_raw, 2, 4, "w1_high", "p m j t")
+        gather_x(1, x_apart[768][:, 1, :], 768, S)
+        gather_x(1, x_apart[BANK][:, 1, :], BANK, 768)
+        x_grouped[768] = keep.tile([P, PACK * 256], BF16, name="x_grouped_3", align_bytes=64)
+        weave(nc.vector.tensor_copy, I32, 768, 0, 256)
+        one = keep.tile([P, 1], F32, name="one", tag="one", align_bytes=64)
+        unit = keep.tile([P, 1], F32, name="unit", tag="unit", align_bytes=64)
+        zero = keep.tile([P, 1], F32, name="zero", tag="zero", align_bytes=64)
+        nc.gpsimd.memset(one[:], 1.0)
+        nc.gpsimd.memset(unit[:], 1.0)
+        nc.gpsimd.memset(zero[:], 0.0)
+
+        def copy_times_one(out, in_):
+            nc.scalar.activation(out=out, in_=in_, func=COPY, scale=one[:])
+
+        def copy_times_unit(out, in_):
+            nc.gpsimd.tensor_scalar(out=out, in0=in_, scalar1=unit[:], scalar2=zero[:], op0=MULT, op1=ADD)
+
+        w1_first = keep.tile([P, 2 * PACK * P], BF16, name="w1_first", align_bytes=64)
+        deal_w(copy_times_unit, w1_first[:], w1_raw, 0, 2, "p m t j", slice(0, 64))
+        deal_w(copy_times_one, w1_first[:], w1_raw, 0, 2, "p m j t", slice(64, P))
+        x_grouped[BANK] = keep.tile([P, PACK * 256], BF16, name="x_grouped_2", tag="one", align_bytes=64)
+        weave(nc.scalar.copy, U32, BANK, 0, 256)
+        w1_high = cast_w(nc.scalar.copy, "y", w1_raw, 2, 4, "x_apart_512", "p m j t")
+        quantize_w("y", w1_first, 0, 0, 1, "codes_y0")
+        x_codes[0] = keep.tile([P, BANK], U32, name="x_codes_0", tag="unit", align_bytes=64)
         quantize_x(0, 0, BANK)
-        x_grouped.append(keep.tile([P, PACK * BANK], BF16, name="x_grouped_1", tag="x_apart_0", align_bytes=64))
-        weave(nc.vector.tensor_copy, I32, 1, 0, BANK)
-        quantize_w("y", w1_first, 0, 0, 2, "codes_y0")
-        x_codes.append(keep.tile([P, BANK], U32, name="x_codes_1", tag="w1_first", align_bytes=64))
-        quantize_x(1, 0, 256)
+        x_codes[1] = keep.tile([P, BANK], U32, name="x_codes_1", tag="zero", align_bytes=64)
         quantize_x(1, 256, BANK)
-        product("y", 0, ((0, 0, BANK, nc.vector.tensor_copy), (1, 0, 256, nc.scalar.copy), (1, 256, BANK, nc.scalar.copy)))
+        quantize_x(1, 0, 256)
+        quantize_w("y", w1_first, 0, 1, 2, "codes_y1")
+        product("y", 0, ((0, 0, BANK, nc.vector.tensor_copy), (1, 256, BANK, nc.scalar.copy), (1, 0, 256, nc.scalar.copy)))
         quantize_w("y", w1_high, 2, 2, 4, "shared_h")
 
         gate = [keep.tile([P, U], F32, name="gate_%d" % t) for t in range(PACK)]
@@ -202,11 +226,11 @@ def tile_picked_edgeatt_sigmoid_lo_kernel(
         product("y", 2)
         last_banks = [multiply("y", 3, h, 0, BANK) for h in range(2)]
         w2_grouped = keep.tile([P, PACK * PACK * P], BF16, name="w_grouped_e", tag="shared_h", align_bytes=64)
-        deal_w(rounding_copy, w2_grouped[:, : 2 * PACK * P], w2_raw, 0, 2, "p t m j")
+        deal_w(rounding_copy, w2_grouped[:, : 2 * PACK * P], w2_raw, 0, 2, "p m t j")
         deal_w(nc.scalar.copy, w2_grouped[:, 2 * PACK * P :], w2_raw, 2, PACK, "p m j t")
         for h in range(2):
             nc.scalar.copy(out=results["y", 3][:, h * BANK : (h + 1) * BANK], in_=last_banks[h][:])
-        w3_grouped = cast_w(nc.scalar.copy, "h", w3_raw, 0, PACK, "w1_high", "p m j t")
+        w3_grouped = cast_w(nc.scalar.copy, "h", w3_raw, 0, PACK, "x_apart_512", "p m j t")
         gather_y(0)
         gather_y(1)
         gather_y(2)

@@ -30,7 +30,7 @@ def tile_picked_edgeatt_sigmoid_lo_kernel(
     with ExitStack() as ctx:
         lists = ctx.enter_context(tc.tile_pool(name="lists", bufs=1))
         keep = ctx.enter_context(tc.tile_pool(name="keep", bufs=1))
-        psum = ctx.enter_context(tc.psum_pool(name="psum", bufs=8))
+        psum = ctx.enter_context(tc.psum_pool(name="psum", bufs=1))
 
         offs_sb = lists.tile([P, S // STRIPE], U16, name="offs_sb")
         src_sb = lists.tile([P, U // STRIPE], U16, name="src_sb")
@@ -134,19 +134,19 @@ def tile_picked_edgeatt_sigmoid_lo_kernel(
                 w_codes[n, t] = codes[:, (t - lo) * P : (t - lo + 1) * P]
                 w_scales[n, t] = scales[:, (t - lo) * P : (t - lo + 1) * P]
 
-        widths = {"y": S + 352, "e": S + 16, "h": S}
+        widths = {"y": S + 16, "e": S + 16, "h": S + 16}
         results = {
             (n, t): keep.tile([P, widths[n]], F32, name="result_%s_%d" % (n, t)) for n in "yeh" for t in range(PACK)
         }
-        for n in "ye":
+        for n in "yeh":
             for t in range(PACK):
                 nc.gpsimd.memset(results[n, t][:, S:], 0.0)
 
         warm = keep.tile([P, 1], F32, name="warm")
         nc.scalar.activation(out=warm[:], in_=results["y", 0][:, S : S + 1], func=SIGMOID)
 
-        def multiply(n, t, h, lo, hi):
-            acc = psum.tile([P, hi - lo], F32, name="acc")
+        def multiply(n, t, h, lo, hi, bank):
+            acc = psum.tile([P, hi - lo], F32, name="acc_%s_%d_%d_%d" % (n, t, h, lo), tag="bank_%d" % bank)
             nc.tensor.matmul_mx(
                 out=acc[:],
                 lhsT=w_codes[n, t].bitcast(FP8X4),
@@ -158,10 +158,13 @@ def tile_picked_edgeatt_sigmoid_lo_kernel(
             )
             return acc
 
-        def product(n, t, pieces=((0, 0, BANK, nc.scalar.copy), (1, 0, BANK, nc.scalar.copy))):
-            for h, lo, hi, copy in pieces:
-                acc = multiply(n, t, h, lo, hi)
-                copy(out=results[n, t][:, h * BANK + lo : h * BANK + hi], in_=acc[:])
+        def product(n, t, copy, banks):
+            for h in range(2):
+                piece(n, t, h, 0, BANK, copy, banks[h])
+
+        def piece(n, t, h, lo, hi, copy, bank):
+            acc = multiply(n, t, h, lo, hi, bank)
+            copy(out=results[n, t][:, h * BANK + lo : h * BANK + hi], in_=acc[:])
 
         def cast_shared(a, lo, cut, hi):
             cast_x(nc.scalar.copy, a, lo, cut)
@@ -209,69 +212,48 @@ def tile_picked_edgeatt_sigmoid_lo_kernel(
         quantize_x(1, 256, BANK)
         quantize_x(1, 0, 256)
         quantize_w("y", w1_first, 0, 1, 2, "codes_y1")
-        product("y", 0, ((0, 0, BANK, nc.vector.tensor_copy), (1, 256, BANK, nc.scalar.copy), (1, 0, 256, nc.scalar.copy)))
-        quantize_w("y", w1_high, 2, 2, 4, "shared_h")
+        piece("y", 0, 0, 0, BANK, nc.vector.tensor_copy, 0)
+        piece("y", 0, 1, 256, BANK, nc.scalar.copy, 1)
+        piece("y", 0, 1, 0, 256, nc.scalar.copy, 2)
+        quantize_w("y", w1_high, 2, 2, 4, "codes_y2")
 
         gate = [keep.tile([P, U], F32, name="gate_%d" % t) for t in range(PACK)]
-
-        def gather_y(t):
-            nc.vector.tensor_copy(out=gate[t][:], in_=results["y", t][:].indirect(dst_sb[:]))
-
-        def gather_e(t):
-            both = keep.tile([P, U], F32, name="both_%d" % t, tag="both_%d" % t)
-            nc.vector.tensor_tensor(out=both[:], in0=results["e", t][:].indirect(src_sb[:]), in1=gate[t][:], op=ADD)
-            nc.scalar.activation(out=gate[t][:], in_=both[:], func=SIGMOID)
-
-        product("y", 1)
-        product("y", 2)
-        last_banks = [multiply("y", 3, h, 0, BANK) for h in range(2)]
-        w2_grouped = keep.tile([P, PACK * PACK * P], BF16, name="w_grouped_e", tag="shared_h", align_bytes=64)
-        deal_w(rounding_copy, w2_grouped[:, : 2 * PACK * P], w2_raw, 0, 2, "p m t j")
-        deal_w(nc.scalar.copy, w2_grouped[:, 2 * PACK * P :], w2_raw, 2, PACK, "p m j t")
-        for h in range(2):
-            nc.scalar.copy(out=results["y", 3][:, h * BANK : (h + 1) * BANK], in_=last_banks[h][:])
-        w3_grouped = cast_w(nc.scalar.copy, "h", w3_raw, 0, PACK, "x_apart_512", "p m j t")
-        gather_y(0)
-        gather_y(1)
-        gather_y(2)
-        quantize_w("e", w2_grouped, 0, 0, PACK, "codes_e")
-        gather_y(3)
-        quantize_w("h", w3_grouped, 0, 0, PACK, "codes_h")
-        for n in "eh":
-            for t in range(PACK):
-                product(n, t)
-        for t in range(PACK):
-            gather_e(t)
-
+        both = [keep.tile([P, U], F32, name="both_%d" % t) for t in range(PACK)]
+        messages = keep.tile([P, PACK * U], F32, name="messages")[:].rearrange("p (t c) -> p t c", t=PACK)
         out_words = keep.tile([P, U], U32, name="out_words", align_bytes=64)
         out_scales = keep.tile([P, U], U8, name="out_scales", align_bytes=64)
         out_grouped = keep.tile([P, PACK * U], BF16, name="out_grouped", align_bytes=64)
         out_rows = out_0.rearrange("(p t) c -> p t c", t=PACK)
         words_hbm = out_1[0].rearrange("p c r -> p (c r)").bitcast(I32)
         scales_hbm = out_2[0].bitcast(I32)
+        on_vector, on_scalar = nc.vector.tensor_copy, nc.scalar.copy
 
-        early = keep.tile([P, PACK, 512], F32, name="early")
-        late = keep.tile([P, PACK, 512], F32, name="late", tag="both_3")
+        def gather_y(t, lo=0, hi=U):
+            window = results["y", t][:].indirect(entries(dst_sb, lo, hi))
+            nc.scalar.activation(out=gate[t][:, lo:hi], in_=window, func=COPY)
 
-        def messages(tiles, lo, hi):
-            held, first = (early, 0) if lo < 512 else (late, 512)
-            return held[:, tiles, lo - first : hi - first]
+        def gather_e(t, lo=0, hi=U):
+            window = results["e", t][:].indirect(entries(src_sb, lo, hi))
+            nc.vector.tensor_tensor(out=both[t][:, lo:hi], in0=window, in1=gate[t][:, lo:hi], op=ADD)
+
+        def sigmoid(t, lo=0, hi=U):
+            nc.scalar.activation(out=gate[t][:, lo:hi], in_=both[t][:, lo:hi], func=SIGMOID)
 
         def gather_h(t, lo, hi):
             nc.vector.tensor_tensor(
-                out=messages(t, lo, hi),
+                out=messages[:, t, lo:hi],
                 in0=results["h", t][:].indirect(entries(src_sb, lo, hi)),
                 in1=gate[t][:, lo:hi],
                 op=MULT,
             )
 
         def store_messages(t, lo, hi):
-            nc.sync.dma_start(out=out_rows[:, t : t + 2, lo:hi], in_=messages(slice(t, t + 2), lo, hi))
+            nc.sync.dma_start(out=out_rows[:, t, lo:hi], in_=messages[:, t, lo:hi])
 
-        def interleave(lo, hi):
-            nc.scalar.copy(
+        def interleave(copy, lo, hi):
+            copy(
                 out=out_grouped[:, PACK * lo : PACK * hi].rearrange("p (c i t) -> p c t i", i=4, t=PACK),
-                in_=messages(slice(0, PACK), lo, hi).rearrange("p t (c i) -> p c t i", i=4),
+                in_=messages[:, :, lo:hi].rearrange("p t (c i) -> p c t i", i=4),
             )
 
         def quantize_out(lo, hi):
@@ -284,26 +266,58 @@ def tile_picked_edgeatt_sigmoid_lo_kernel(
         def store_words(lo, hi):
             nc.sync.dma_start(out=words_hbm[:, lo:hi], in_=out_words[:, lo:hi].bitcast(I32))
 
-        for t in (0, 2):
-            gather_h(t, 0, 512)
-            gather_h(t + 1, 0, 512)
-            store_messages(t, 0, 512)
-        interleave(0, 512)
-        for t in (0, 2):
-            gather_h(t, 512, 768)
-            gather_h(t + 1, 512, 768)
-        store_messages(2, 512, 768)
-        interleave(512, 768)
-        gather_h(0, 768, U)
-        gather_h(1, 768, U)
-        store_messages(0, 512, U)
-        for lo, hi in ((768, 896), (896, U)):
+        def round_w(n, raw):
+            grouped = keep.tile([P, PACK * PACK * P], BF16, name="w_grouped_" + n, align_bytes=64)
+            for rows in (slice(0, 64), slice(64, P)):
+                deal_w(rounding_copy, grouped[:], raw, 0, PACK, "p m t j", rows)
+            quantize_w(n, grouped, 0, 0, PACK, "codes_" + n)
+
+        gather_y(0)
+        product("y", 1, on_vector, (3, 4))
+        gather_y(1)
+        round_w("e", w2_raw)
+        product("y", 2, on_vector, (5, 6))
+        product("e", 0, on_vector, (7, 0))
+        product("e", 1, on_scalar, (1, 2))
+        round_w("h", w3_raw)
+        gather_y(2)
+        gather_e(0)
+        sigmoid(0)
+        product("h", 0, on_scalar, (3, 4))
+        gather_e(1)
+        product("e", 2, on_vector, (5, 6))
+        sigmoid(1)
+        gather_e(2)
+        product("h", 1, on_scalar, (7, 0))
+        product("y", 3, on_scalar, (1, 2))
+        gather_h(0, 0, U)
+        store_messages(0, 0, U)
+        sigmoid(2, 0, 512)
+        product("e", 3, on_scalar, (3, 4))
+        gather_h(1, 0, U)
+        store_messages(1, 0, U)
+        gather_y(3, 0, 512)
+        gather_e(3, 0, 512)
+        product("h", 2, on_scalar, (7, 0))
+        product("h", 3, on_scalar, (1, 2))
+        sigmoid(3, 0, 512)
+        gather_y(3, 512, U)
+        gather_h(2, 0, 512)
+        gather_h(3, 0, 512)
+        nc.sync.dma_start(out=out_rows[:, 2:4, 0:512], in_=messages[:, 2:4, 0:512])
+        sigmoid(2, 512, U)
+        gather_e(3, 512, U)
+        interleave(on_scalar, 0, 256)
+        sigmoid(3, 512, U)
+        interleave(on_scalar, 256, 512)
+        for lo, hi in ((512, 768), (768, U)):
             gather_h(2, lo, hi)
             gather_h(3, lo, hi)
-            interleave(lo, hi)
-        store_messages(2, 768, U)
+            nc.sync.dma_start(out=out_rows[:, 2:4, lo:hi], in_=messages[:, 2:4, lo:hi])
+        interleave(on_scalar, 512, 768)
         quantize_out(0, 512)
         store_words(0, 512)
+        interleave(on_vector, 768, U)
         quantize_out(512, 768)
         store_words(512, 768)
         quantize_out(768, U)

@@ -266,26 +266,26 @@ def tile_picked_edgeatt_sigmoid_lo_kernel(
         def store_words(lo, hi):
             nc.sync.dma_start(out=words_hbm[:, lo:hi], in_=out_words[:, lo:hi].bitcast(I32))
 
-        def round_w(n, raw):
-            grouped = keep.tile([P, PACK * PACK * P], BF16, name="w_grouped_" + n, align_bytes=64)
-            for rows in (slice(0, 64), slice(64, P)):
-                deal_w(rounding_copy, grouped[:], raw, 0, PACK, "p m t j", rows)
-            quantize_w(n, grouped, 0, 0, PACK, "codes_" + n)
-
         gather_y(0)
         product("y", 1, on_vector, (3, 4))
         gather_y(1)
-        round_w("e", w2_raw)
-        product("y", 2, on_vector, (5, 6))
+        w2_low = cast_w(rounding_copy, "e", w2_raw, 0, 2, "w2_low", "p m t j")
+        w2_high = cast_w(on_vector, "e", w2_raw, 2, PACK, "w2_high", "p m j t")
+        quantize_w("e", w2_low, 0, 0, 2, "codes_e0")
+        quantize_w("e", w2_high, 2, 2, PACK, "codes_e2")
+        w3_grouped = cast_w(on_vector, "h", w3_raw, 0, PACK, "w3_grouped", "p m j t")
         product("e", 0, on_vector, (7, 0))
+        piece("y", 2, 0, 0, BANK, on_vector, 5)
+        quantize_w("h", w3_grouped, 0, 0, PACK, "codes_h")
         product("e", 1, on_scalar, (1, 2))
-        round_w("h", w3_raw)
+        piece("y", 2, 1, 0, BANK, on_scalar, 6)
         gather_y(2)
         gather_e(0)
         sigmoid(0)
         product("h", 0, on_scalar, (3, 4))
         gather_e(1)
-        product("e", 2, on_vector, (5, 6))
+        piece("e", 2, 0, 0, BANK, on_scalar, 5)
+        piece("e", 2, 1, 0, BANK, on_scalar, 6)
         sigmoid(1)
         gather_e(2)
         product("h", 1, on_scalar, (7, 0))

@@ -21,6 +21,7 @@ P = 128
 PACK = 4
 BANK = 512
 STRIPE = 16
+SPARE = 16
 
 
 def tile_picked_edgeatt_sigmoid_lo_kernel(
@@ -31,6 +32,7 @@ def tile_picked_edgeatt_sigmoid_lo_kernel(
         lists = ctx.enter_context(tc.tile_pool(name="lists", bufs=1))
         keep = ctx.enter_context(tc.tile_pool(name="keep", bufs=1))
         psum = ctx.enter_context(tc.psum_pool(name="psum", bufs=1))
+        on_vector, on_scalar = nc.vector.tensor_copy, nc.scalar.copy
 
         offs_sb = lists.tile([P, S // STRIPE], U16, name="offs_sb")
         src_sb = lists.tile([P, U // STRIPE], U16, name="src_sb")
@@ -40,90 +42,69 @@ def tile_picked_edgeatt_sigmoid_lo_kernel(
             return list_sb[:, lo // STRIPE : hi // STRIPE]
 
         x_rows = xT.rearrange("(p j) c -> p j c", j=PACK)
+        planes = [keep.tile([P, T], F32, name="plane_%d" % j) for j in range(PACK)]
 
-        pieces = {0: (0, 1280), 1: (1280, T), 2: (0, 768), 3: (768, 1408), 4: (1408, 1792), 5: (1792, T)}
-        x_raw = {key: keep.tile([P, 2, hi - lo], F32, name="x_raw_%d" % key) for key, (lo, hi) in pieces.items()}
-
-        def load_x(key, rows, lo, hi):
-            first = pieces[key][0]
-            into = x_raw[key][:, rows[0] % 2 : rows[-1] % 2 + 1, lo - first : hi - first]
-            nc.sync.dma_start(out=into, in_=x_rows[:, rows[0] : rows[-1] + 1, lo:hi])
-
-        def load_w(w, label, lo, hi):
-            raw = keep.tile([P, PACK, hi - lo], F32, name="w_raw_%s_%d" % (label, lo))
-            nc.sync.dma_start(out=raw[:], in_=w.rearrange("(p j) c -> p j c", j=PACK)[:, :, lo:hi])
+        def load_w(w, label):
+            raw = keep.tile([P, PACK, N], F32, name="w_raw_%s" % label)
+            nc.sync.dma_start(out=raw[:], in_=w.rearrange("(p j) c -> p j c", j=PACK))
             return raw
 
-        load_x(0, (0, 1), 0, 1280)
+        nc.sync.dma_start(out=planes[0][:], in_=x_rows[:, 0, :])
         nc.sync.dma_start(offs_sb[:], offs)
-        load_x(1, (0, 1), 1280, T)
-        for key in range(2, 6):
-            load_x(key, (2, 3), *pieces[key])
-        w1_raw = load_w(w1, "y", 0, N)
+        for j in range(1, PACK):
+            nc.sync.dma_start(out=planes[j][:], in_=x_rows[:, j, :])
+        w1_raw = load_w(w1, "y")
         nc.sync.dma_start(dst_sb[:], dst)
-        w2_raw = load_w(w2, "e", 0, N)
+        w2_raw = load_w(w2, "e")
         nc.sync.dma_start(src_sb[:], src)
-        w3_raw = load_w(w3, "h", 0, N)
+        w3_raw = load_w(w3, "h")
 
-        pairs = [keep.tile([P, 2 * T], BF16, name="pairs_%d" % a, align_bytes=64) for a in range(2)]
-
-        def cast_x(copy, key, lo, hi):
-            a, first = min(key // 2, 1), pieces[key][0]
-            copy(
-                out=pairs[a][:, 2 * lo : 2 * hi].rearrange("p (c i j) -> p c j i", i=4, j=2),
-                in_=x_raw[key][:, :, lo - first : hi - first].rearrange("p j (c i) -> p c j i", i=4),
-            )
-
-        x_grouped = {0: keep.tile([P, PACK * BANK], BF16, name="x_grouped_0", align_bytes=64)}
+        picked = [keep.tile([P, 2 * S], BF16, name="picked_%d" % a, tag="picked_%d" % a, align_bytes=64) for a in range(2)]
+        x_grouped = keep.tile([P, PACK * S], BF16, name="x_grouped", align_bytes=64)
         x_codes = {}
-        x_scales = [keep.tile([P, BANK], U8, name="x_scales_%d" % h, align_bytes=64) for h in range(2)]
+        x_scales = {}
 
-        x_apart = {
-            lo: keep.tile([P, 2, hi - lo], U32, name="x_apart_%d" % lo, tag="x_apart_%d" % lo, align_bytes=64)
-            for lo, hi in ((0, BANK), (BANK, 768), (768, S))
-        }
+        def gather_x(engine, j, lo, hi):
+            row = picked[j // 2][:, (j % 2) * S + lo : (j % 2) * S + hi]
+            window = planes[j][:].indirect(entries(offs_sb, lo, hi))
+            if engine == "vector":
+                nc.vector.tensor_copy(out=row, in_=window)
+            else:
+                nc.scalar.activation(out=row, in_=window, func=COPY)
 
-        def weave(copy, dtype, first, lo, hi):
-            words = x_grouped[first][:].bitcast(dtype)[:, 2 * lo : 2 * hi]
-            rows = x_apart[first][:].rearrange("p a s -> p (a s)").bitcast(dtype).rearrange("p (a s) -> p a s", a=2)
-            copy(
-                out=words.rearrange("p (c i a) -> p c a i", i=2, a=2),
-                in_=rows[:, :, lo:hi].rearrange("p a (c i) -> p c a i", i=2),
-            )
+        def place_x(a, lo, hi):
+            slots = x_grouped[:].rearrange("p (c a j) -> p c a j", a=2, j=2)[:, lo:hi, a, :]
+            rows = picked[a][:].rearrange("p (j c) -> p c j", j=2)[:, lo:hi, :]
+            nc.vector.tensor_copy(out=slots, in_=rows)
 
-        def gather_x(a, out, lo, hi):
-            nc.vector.tensor_copy(out=out, in_=pairs[a][:].bitcast(U32).indirect(entries(offs_sb, lo, hi)))
-
-        def quantize_x(h, lo, hi):
-            first = h * BANK + lo
+        def quantize_x(lo, hi, tag):
+            x_codes[lo] = keep.tile([P, hi - lo], U32, name="x_codes_%d" % lo, tag=tag, align_bytes=64)
+            x_scales[lo] = keep.tile([P, hi - lo], U8, name="x_scales_%d" % lo, align_bytes=64)
             nc.vector.quantize_mx(
-                out=x_codes[h][:, lo:hi].bitcast(FP8X4),
-                scales=x_scales[h][:, lo:hi],
-                in_=x_grouped[first][:],
+                out=x_codes[lo][:].bitcast(FP8X4),
+                scales=x_scales[lo][:],
+                in_=x_grouped[:, PACK * lo : PACK * hi],
             )
 
         w_codes = {}
         w_scales = {}
 
-        def rounding_copy(out, in_):
+        def on_gpsimd(out, in_):
             nc.gpsimd.tensor_scalar(out=out, in0=in_, scalar1=1.0, scalar2=0.0, op0=MULT, op1=ADD)
-
-        def deal_w(copy, grouped, raw, lo, hi, walk, rows=slice(0, P)):
-            dealt = raw[:].rearrange("p j (m t) -> p j m t", t=PACK)[:, :, rows, lo:hi]
-            copy(
-                out=grouped.rearrange("p (t m j) -> p t m j", m=P, j=PACK)[:, :, rows, :].rearrange("p t m j -> " + walk),
-                in_=dealt.rearrange("p j m t -> " + walk),
-            )
 
         def cast_w(copy, n, raw, lo, hi, tag, walk):
             grouped = keep.tile(
                 [P, (hi - lo) * PACK * P], BF16, name="w_grouped_%s_%d" % (n, lo), tag=tag, align_bytes=64
             )
-            deal_w(copy, grouped[:], raw, lo, hi, walk)
+            dealt = raw[:].rearrange("p j (m t) -> p j m t", t=PACK)[:, :, :, lo:hi]
+            copy(
+                out=grouped[:].rearrange("p (t m j) -> p t m j", m=P, j=PACK).rearrange("p t m j -> " + walk),
+                in_=dealt.rearrange("p j m t -> " + walk),
+            )
             return grouped
 
-        def quantize_w(n, grouped, first, lo, hi, tag):
-            codes = keep.tile([P, (hi - lo) * P], U32, name="w_codes_%s_%d" % (n, lo), tag=tag, align_bytes=64)
+        def quantize_w(n, grouped, first, lo, hi):
+            codes = keep.tile([P, (hi - lo) * P], U32, name="w_codes_%s_%d" % (n, lo), align_bytes=64)
             scales = keep.tile([P, (hi - lo) * P], U8, name="w_scales_%s_%d" % (n, lo), align_bytes=64)
             nc.vector.quantize_mx(
                 out=codes[:].bitcast(FP8X4),
@@ -134,9 +115,8 @@ def tile_picked_edgeatt_sigmoid_lo_kernel(
                 w_codes[n, t] = codes[:, (t - lo) * P : (t - lo + 1) * P]
                 w_scales[n, t] = scales[:, (t - lo) * P : (t - lo + 1) * P]
 
-        widths = {"y": S + 16, "e": S + 16, "h": S + 16}
         results = {
-            (n, t): keep.tile([P, widths[n]], F32, name="result_%s_%d" % (n, t)) for n in "yeh" for t in range(PACK)
+            (n, t): keep.tile([P, S + SPARE], F32, name="result_%s_%d" % (n, t)) for n in "yeh" for t in range(PACK)
         }
         for n in "yeh":
             for t in range(PACK):
@@ -145,77 +125,25 @@ def tile_picked_edgeatt_sigmoid_lo_kernel(
         warm = keep.tile([P, 1], F32, name="warm")
         nc.scalar.activation(out=warm[:], in_=results["y", 0][:, S : S + 1], func=SIGMOID)
 
-        def multiply(n, t, h, lo, hi, bank):
-            acc = psum.tile([P, hi - lo], F32, name="acc_%s_%d_%d_%d" % (n, t, h, lo), tag="bank_%d" % bank)
-            nc.tensor.matmul_mx(
-                out=acc[:],
-                lhsT=w_codes[n, t].bitcast(FP8X4),
-                lhsT_scale=w_scales[n, t],
-                rhs=x_codes[h][:, lo:hi].bitcast(FP8X4),
-                rhs_scale=x_scales[h][:, lo:hi],
-                start=True,
-                stop=True,
-            )
-            return acc
+        def piece(n, t, lo, hi, copy, bank):
+            acc = psum.tile([P, hi - lo], F32, name="acc_%s_%d_%d" % (n, t, lo), tag="bank_%d" % bank)
+            for first in sorted(x_codes):
+                if lo <= first < hi:
+                    width = x_codes[first].shape[1]
+                    nc.tensor.matmul_mx(
+                        out=acc[:, first - lo : first - lo + width],
+                        lhsT=w_codes[n, t].bitcast(FP8X4),
+                        lhsT_scale=w_scales[n, t],
+                        rhs=x_codes[first][:].bitcast(FP8X4),
+                        rhs_scale=x_scales[first][:],
+                        start=True,
+                        stop=True,
+                    )
+            copy(out=results[n, t][:, lo:hi], in_=acc[:])
 
         def product(n, t, copy, banks):
             for h in range(2):
-                piece(n, t, h, 0, BANK, copy, banks[h])
-
-        def piece(n, t, h, lo, hi, copy, bank):
-            acc = multiply(n, t, h, lo, hi, bank)
-            copy(out=results[n, t][:, h * BANK + lo : h * BANK + hi], in_=acc[:])
-
-        def cast_shared(a, lo, cut, hi):
-            cast_x(nc.scalar.copy, a, lo, cut)
-            cast_x(nc.vector.tensor_copy, a, cut, hi)
-
-        cast_shared(0, 0, 416, 1280)
-        cast_shared(1, 1280, 1504, T)
-        gather_x(0, x_apart[0][:, 0, :], 0, BANK)
-        gather_x(0, x_apart[BANK][:, 0, :], BANK, 768)
-        gather_x(0, x_apart[768][:, 0, :], 768, S)
-        cast_x(nc.scalar.copy, 2, *pieces[2])
-        cast_shared(3, 768, 1120, 1408)
-        cast_x(nc.vector.tensor_copy, 4, *pieces[4])
-        cast_shared(5, 1792, 1872, T)
-        for lo, hi in ((0, 256), (256, BANK)):
-            gather_x(1, x_apart[0][:, 1, lo:hi], lo, hi)
-            weave(nc.scalar.copy, U32, 0, lo, hi)
-        gather_x(1, x_apart[768][:, 1, :], 768, S)
-        gather_x(1, x_apart[BANK][:, 1, :], BANK, 768)
-        x_grouped[768] = keep.tile([P, PACK * 256], BF16, name="x_grouped_3", align_bytes=64)
-        weave(nc.vector.tensor_copy, I32, 768, 0, 256)
-        one = keep.tile([P, 1], F32, name="one", tag="one", align_bytes=64)
-        unit = keep.tile([P, 1], F32, name="unit", tag="unit", align_bytes=64)
-        zero = keep.tile([P, 1], F32, name="zero", tag="zero", align_bytes=64)
-        nc.gpsimd.memset(one[:], 1.0)
-        nc.gpsimd.memset(unit[:], 1.0)
-        nc.gpsimd.memset(zero[:], 0.0)
-
-        def copy_times_one(out, in_):
-            nc.scalar.activation(out=out, in_=in_, func=COPY, scale=one[:])
-
-        def copy_times_unit(out, in_):
-            nc.gpsimd.tensor_scalar(out=out, in0=in_, scalar1=unit[:], scalar2=zero[:], op0=MULT, op1=ADD)
-
-        w1_first = keep.tile([P, 2 * PACK * P], BF16, name="w1_first", align_bytes=64)
-        deal_w(copy_times_unit, w1_first[:], w1_raw, 0, 2, "p m t j", slice(0, 64))
-        deal_w(copy_times_one, w1_first[:], w1_raw, 0, 2, "p m j t", slice(64, P))
-        x_grouped[BANK] = keep.tile([P, PACK * 256], BF16, name="x_grouped_2", tag="one", align_bytes=64)
-        weave(nc.scalar.copy, U32, BANK, 0, 256)
-        w1_high = cast_w(nc.scalar.copy, "y", w1_raw, 2, 4, "x_apart_512", "p m j t")
-        quantize_w("y", w1_first, 0, 0, 1, "codes_y0")
-        x_codes[0] = keep.tile([P, BANK], U32, name="x_codes_0", tag="unit", align_bytes=64)
-        quantize_x(0, 0, BANK)
-        x_codes[1] = keep.tile([P, BANK], U32, name="x_codes_1", tag="zero", align_bytes=64)
-        quantize_x(1, 256, BANK)
-        quantize_x(1, 0, 256)
-        quantize_w("y", w1_first, 0, 1, 2, "codes_y1")
-        piece("y", 0, 0, 0, BANK, nc.vector.tensor_copy, 0)
-        piece("y", 0, 1, 256, BANK, nc.scalar.copy, 1)
-        piece("y", 0, 1, 0, 256, nc.scalar.copy, 2)
-        quantize_w("y", w1_high, 2, 2, 4, "codes_y2")
+                piece(n, t, h * BANK, (h + 1) * BANK, copy, banks[h])
 
         gate = [keep.tile([P, U], F32, name="gate_%d" % t) for t in range(PACK)]
         both = [keep.tile([P, U], F32, name="both_%d" % t) for t in range(PACK)]
@@ -226,11 +154,14 @@ def tile_picked_edgeatt_sigmoid_lo_kernel(
         out_rows = out_0.rearrange("(p t) c -> p t c", t=PACK)
         words_hbm = out_1[0].rearrange("p c r -> p (c r)").bitcast(I32)
         scales_hbm = out_2[0].bitcast(I32)
-        on_vector, on_scalar = nc.vector.tensor_copy, nc.scalar.copy
 
         def gather_y(t, lo=0, hi=U):
             window = results["y", t][:].indirect(entries(dst_sb, lo, hi))
             nc.scalar.activation(out=gate[t][:, lo:hi], in_=window, func=COPY)
+
+        def gather_y_on_vector(t, lo=0, hi=U):
+            window = results["y", t][:].indirect(entries(dst_sb, lo, hi))
+            nc.vector.tensor_copy(out=gate[t][:, lo:hi], in_=window)
 
         def gather_e(t, lo=0, hi=U):
             window = results["e", t][:].indirect(entries(src_sb, lo, hi))
@@ -247,8 +178,8 @@ def tile_picked_edgeatt_sigmoid_lo_kernel(
                 op=MULT,
             )
 
-        def store_messages(t, lo, hi):
-            nc.sync.dma_start(out=out_rows[:, t, lo:hi], in_=messages[:, t, lo:hi])
+        def store_messages(first, last, lo, hi):
+            nc.sync.dma_start(out=out_rows[:, first:last, lo:hi], in_=messages[:, first:last, lo:hi])
 
         def interleave(copy, lo, hi):
             copy(
@@ -266,36 +197,67 @@ def tile_picked_edgeatt_sigmoid_lo_kernel(
         def store_words(lo, hi):
             nc.sync.dma_start(out=words_hbm[:, lo:hi], in_=out_words[:, lo:hi].bitcast(I32))
 
+        def store_scales():
+            for q in range(4):
+                queue = nc.sync if q % 2 == 0 else nc.scalar
+                queue.dma_start(
+                    out=scales_hbm[4 * q : 4 * q + 4, :], in_=out_scales[32 * q : 32 * q + 4, :].bitcast(I32)
+                )
+
+        for j in range(2):
+            gather_x("vector", j, 0, 512)
+            gather_x("scalar", j, 512, S)
+        place_x(0, 0, S)
+        gather_x("scalar", 2, 256, S)
+        gather_x("vector", 2, 0, 256)
+        gather_x("vector", 3, 0, 256)
+        for lo, hi in ((256, 512), (512, 768), (768, S)):
+            gather_x("scalar", 3, lo, hi)
+        place_x(1, 256, 512)
+        place_x(1, 0, 256)
+        place_x(1, 512, 768)
+        quantize_x(0, 512, "x_codes_0")
+        place_x(1, 768, S)
+        w1_first = cast_w(on_scalar, "y", w1_raw, 0, 1, "w1_first", "p m j t")
+        quantize_x(512, 768, "x_codes_512")
+        quantize_w("y", w1_first, 0, 0, 1)
+        w1_second = cast_w(on_scalar, "y", w1_raw, 1, 2, "w1_second", "p m j t")
+        quantize_x(768, S, "w1_first")
+        quantize_w("y", w1_second, 1, 1, 2)
+        piece("y", 0, 0, 512, on_scalar, 0)
+        piece("y", 0, 512, 768, on_scalar, 1)
+        piece("y", 0, 768, S, on_vector, 2)
+        w1_high = cast_w(on_vector, "y", w1_raw, 2, 4, "w1_second", "p m j t")
+        quantize_w("y", w1_high, 2, 2, 4)
         gather_y(0)
         product("y", 1, on_vector, (3, 4))
         gather_y(1)
-        w2_low = cast_w(rounding_copy, "e", w2_raw, 0, 2, "w2_low", "p m t j")
+        w2_low = cast_w(on_gpsimd, "e", w2_raw, 0, 2, "w2_low", "p m t j")
         w2_high = cast_w(on_vector, "e", w2_raw, 2, PACK, "w2_high", "p m j t")
-        quantize_w("e", w2_low, 0, 0, 2, "codes_e0")
-        quantize_w("e", w2_high, 2, 2, PACK, "codes_e2")
+        quantize_w("e", w2_low, 0, 0, 2)
+        quantize_w("e", w2_high, 2, 2, PACK)
         w3_grouped = cast_w(on_vector, "h", w3_raw, 0, PACK, "w3_grouped", "p m j t")
         product("e", 0, on_vector, (7, 0))
-        piece("y", 2, 0, 0, BANK, on_vector, 5)
-        quantize_w("h", w3_grouped, 0, 0, PACK, "codes_h")
+        piece("y", 2, 0, 512, on_vector, 5)
+        quantize_w("h", w3_grouped, 0, 0, PACK)
         product("e", 1, on_scalar, (1, 2))
-        piece("y", 2, 1, 0, BANK, on_scalar, 6)
+        piece("y", 2, 512, S, on_scalar, 6)
         gather_y(2)
         gather_e(0)
         sigmoid(0)
         product("h", 0, on_scalar, (3, 4))
         gather_e(1)
-        piece("e", 2, 0, 0, BANK, on_scalar, 5)
-        piece("e", 2, 1, 0, BANK, on_scalar, 6)
+        product("e", 2, on_scalar, (5, 6))
         sigmoid(1)
         gather_e(2)
         product("h", 1, on_scalar, (7, 0))
         product("y", 3, on_scalar, (1, 2))
         gather_h(0, 0, U)
-        store_messages(0, 0, U)
+        store_messages(0, 1, 0, U)
         sigmoid(2, 0, 512)
         product("e", 3, on_scalar, (3, 4))
         gather_h(1, 0, U)
-        store_messages(1, 0, U)
+        store_messages(1, 2, 0, U)
         gather_y(3, 0, 512)
         gather_e(3, 0, 512)
         product("h", 2, on_scalar, (7, 0))
@@ -304,7 +266,7 @@ def tile_picked_edgeatt_sigmoid_lo_kernel(
         gather_y(3, 512, U)
         gather_h(2, 0, 512)
         gather_h(3, 0, 512)
-        nc.sync.dma_start(out=out_rows[:, 2:4, 0:512], in_=messages[:, 2:4, 0:512])
+        store_messages(2, 4, 0, 512)
         sigmoid(2, 512, U)
         gather_e(3, 512, U)
         interleave(on_scalar, 0, 256)
@@ -313,7 +275,7 @@ def tile_picked_edgeatt_sigmoid_lo_kernel(
         for lo, hi in ((512, 768), (768, U)):
             gather_h(2, lo, hi)
             gather_h(3, lo, hi)
-            nc.sync.dma_start(out=out_rows[:, 2:4, lo:hi], in_=messages[:, 2:4, lo:hi])
+            store_messages(2, 4, lo, hi)
         interleave(on_scalar, 512, 768)
         quantize_out(0, 512)
         store_words(0, 512)
@@ -322,8 +284,4 @@ def tile_picked_edgeatt_sigmoid_lo_kernel(
         store_words(512, 768)
         quantize_out(768, U)
         store_words(768, U)
-        for q in range(4):
-            queue = nc.sync if q % 2 == 0 else nc.scalar
-            queue.dma_start(
-                out=scales_hbm[4 * q : 4 * q + 4, :], in_=out_scales[32 * q : 32 * q + 4, :].bitcast(I32)
-            )
+        store_scales()

@@ -89,9 +89,6 @@ def tile_picked_edgeatt_sigmoid_lo_kernel(
         w_codes = {}
         w_scales = {}
 
-        def on_gpsimd(out, in_):
-            nc.gpsimd.tensor_scalar(out=out, in0=in_, scalar1=1.0, scalar2=0.0, op0=MULT, op1=ADD)
-
         def cast_w(copy, n, raw, lo, hi, tag, walk):
             grouped = keep.tile(
                 [P, (hi - lo) * PACK * P], BF16, name="w_grouped_%s_%d" % (n, lo), tag=tag, align_bytes=64
@@ -232,10 +229,8 @@ def tile_picked_edgeatt_sigmoid_lo_kernel(
         gather_y(0)
         product("y", 1, on_vector, (3, 4))
         gather_y(1)
-        w2_low = cast_w(on_gpsimd, "e", w2_raw, 0, 2, "w2_low", "p m t j")
-        w2_high = cast_w(on_vector, "e", w2_raw, 2, PACK, "w2_high", "p m j t")
-        quantize_w("e", w2_low, 0, 0, 2)
-        quantize_w("e", w2_high, 2, 2, PACK)
+        w2_grouped = cast_w(on_vector, "e", w2_raw, 0, PACK, "w1_second", "p m j t")
+        quantize_w("e", w2_grouped, 0, 0, PACK)
         w3_grouped = cast_w(on_vector, "h", w3_raw, 0, PACK, "w3_grouped", "p m j t")
         product("e", 0, on_vector, (7, 0))
         piece("y", 2, 0, 512, on_vector, 5)

@@ -60,7 +60,7 @@ def tile_picked_edgeatt_sigmoid_lo_kernel(
         w3_raw = load_w(w3, "h")
 
         picked = [keep.tile([P, 2 * S], BF16, name="picked_%d" % a, tag="picked_%d" % a, align_bytes=64) for a in range(2)]
-        x_grouped = keep.tile([P, PACK * S], BF16, name="x_grouped", align_bytes=64)
+        x_grouped = keep.tile([P, PACK * S], BF16, name="x_grouped", tag="x_grouped", align_bytes=64)
         x_codes = {}
         x_scales = {}
 
@@ -218,63 +218,69 @@ def tile_picked_edgeatt_sigmoid_lo_kernel(
         w1_first = cast_w(on_scalar, "y", w1_raw, 0, 1, "w1_first", "p m j t")
         quantize_x(512, 768, "x_codes_512")
         quantize_w("y", w1_first, 0, 0, 1)
-        w1_second = cast_w(on_scalar, "y", w1_raw, 1, 2, "w1_second", "p m j t")
         quantize_x(768, S, "w1_first")
-        quantize_w("y", w1_second, 1, 1, 2)
+        w1_middle = cast_w(on_scalar, "y", w1_raw, 1, 3, "w1_middle", "p m j t")
+        w1_last = cast_w(on_vector, "y", w1_raw, 3, PACK, "x_grouped", "p m j t")
+        quantize_w("y", w1_middle, 1, 1, 3)
         piece("y", 0, 0, 512, on_scalar, 0)
         piece("y", 0, 512, 768, on_scalar, 1)
         piece("y", 0, 768, S, on_vector, 2)
-        w1_high = cast_w(on_vector, "y", w1_raw, 2, 4, "w1_second", "p m j t")
-        quantize_w("y", w1_high, 2, 2, 4)
         gather_y(0)
+        w2_grouped = cast_w(on_vector, "e", w2_raw, 0, PACK, "w1_middle", "p m j t")
         product("y", 1, on_vector, (3, 4))
+        piece("y", 2, 512, S, on_scalar, 6)
         gather_y(1)
-        w2_grouped = cast_w(on_vector, "e", w2_raw, 0, PACK, "w1_second", "p m j t")
         quantize_w("e", w2_grouped, 0, 0, PACK)
         w3_grouped = cast_w(on_vector, "h", w3_raw, 0, PACK, "w3_grouped", "p m j t")
         product("e", 0, on_vector, (7, 0))
-        piece("y", 2, 0, 512, on_vector, 5)
-        quantize_w("h", w3_grouped, 0, 0, PACK)
         product("e", 1, on_scalar, (1, 2))
-        piece("y", 2, 512, S, on_scalar, 6)
+        piece("y", 2, 0, 512, on_vector, 5)
         gather_y(2)
         gather_e(0)
         sigmoid(0)
-        product("h", 0, on_scalar, (3, 4))
+        quantize_w("h", w3_grouped, 0, 0, PACK)
+        quantize_w("y", w1_last, 3, 3, PACK)
         gather_e(1)
-        product("e", 2, on_scalar, (5, 6))
-        sigmoid(1)
-        gather_e(2)
-        product("h", 1, on_scalar, (7, 0))
-        product("y", 3, on_scalar, (1, 2))
+        product("h", 0, on_scalar, (3, 4))
+        product("h", 1, on_scalar, (5, 6))
+        piece("y", 3, 0, 512, on_vector, 0)
         gather_h(0, 0, U)
         store_messages(0, 1, 0, U)
-        sigmoid(2, 0, 512)
-        product("e", 3, on_scalar, (3, 4))
+        product("e", 2, on_scalar, (3, 4))
+        gather_e(2)
+        sigmoid(1)
         gather_h(1, 0, U)
         store_messages(1, 2, 0, U)
+        piece("y", 3, 512, S, on_scalar, 5)
+        product("e", 3, on_scalar, (6, 3))
         gather_y(3, 0, 512)
         gather_e(3, 0, 512)
-        product("h", 2, on_scalar, (7, 0))
-        product("h", 3, on_scalar, (1, 2))
-        sigmoid(3, 0, 512)
-        gather_y(3, 512, U)
+        sigmoid(2, 0, 512)
+        product("h", 2, on_scalar, (1, 2))
         gather_h(2, 0, 512)
-        gather_h(3, 0, 512)
+        gather_y(3, 512, U)
+        gather_e(3, 512, U)
+        sigmoid(3, 0, 512)
+        product("h", 3, on_scalar, (4, 5))
+        gather_h(3, 0, 256)
+        gather_h(3, 256, 512)
         store_messages(2, 4, 0, 512)
         sigmoid(2, 512, U)
-        gather_e(3, 512, U)
-        interleave(on_scalar, 0, 256)
         sigmoid(3, 512, U)
+        interleave(on_scalar, 0, 256)
         interleave(on_scalar, 256, 512)
-        for lo, hi in ((512, 768), (768, U)):
-            gather_h(2, lo, hi)
-            gather_h(3, lo, hi)
-            store_messages(2, 4, lo, hi)
+        gather_h(2, 512, 768)
+        gather_h(3, 512, 768)
+        store_messages(2, 4, 512, 768)
         interleave(on_scalar, 512, 768)
+        gather_h(2, 768, U)
+        gather_h(3, 896, U)
+        gather_h(3, 768, 896)
+        store_messages(2, 4, 768, U)
+        interleave(on_scalar, 768, 896)
         quantize_out(0, 512)
         store_words(0, 512)
-        interleave(on_vector, 768, U)
+        interleave(on_vector, 896, U)
         quantize_out(512, 768)
         store_words(512, 768)
         quantize_out(768, U)

@@ -210,8 +210,7 @@ def tile_picked_edgeatt_sigmoid_lo_kernel(
         gather_x("vector", 3, 0, 256)
         for lo, hi in ((256, 512), (512, 768), (768, S)):
             gather_x("scalar", 3, lo, hi)
-        place_x(1, 256, 512)
-        place_x(1, 0, 256)
+        place_x(1, 0, 512)
         place_x(1, 512, 768)
         quantize_x(0, 512, "x_codes_0")
         place_x(1, 768, S)
@@ -219,16 +218,15 @@ def tile_picked_edgeatt_sigmoid_lo_kernel(
         quantize_x(512, 768, "x_codes_512")
         quantize_w("y", w1_first, 0, 0, 1)
         quantize_x(768, S, "w1_first")
-        w1_middle = cast_w(on_scalar, "y", w1_raw, 1, 3, "w1_middle", "p m j t")
-        w1_last = cast_w(on_vector, "y", w1_raw, 3, PACK, "x_grouped", "p m j t")
-        quantize_w("y", w1_middle, 1, 1, 3)
+        w1_rest = cast_w(on_scalar, "y", w1_raw, 1, PACK, "w1_rest", "p m j t")
         piece("y", 0, 0, 512, on_scalar, 0)
         piece("y", 0, 512, 768, on_scalar, 1)
-        piece("y", 0, 768, S, on_vector, 2)
+        piece("y", 0, 768, S, on_scalar, 2)
+        quantize_w("y", w1_rest, 1, 1, PACK)
         gather_y(0)
-        w2_grouped = cast_w(on_vector, "e", w2_raw, 0, PACK, "w1_middle", "p m j t")
+        w2_grouped = cast_w(on_vector, "e", w2_raw, 0, PACK, "w2_grouped", "p m j t")
         product("y", 1, on_vector, (3, 4))
-        piece("y", 2, 512, S, on_scalar, 6)
+        piece("y", 2, 512, S, on_vector, 6)
         gather_y(1)
         quantize_w("e", w2_grouped, 0, 0, PACK)
         w3_grouped = cast_w(on_vector, "h", w3_raw, 0, PACK, "w3_grouped", "p m j t")
@@ -239,7 +237,6 @@ def tile_picked_edgeatt_sigmoid_lo_kernel(
         gather_e(0)
         sigmoid(0)
         quantize_w("h", w3_grouped, 0, 0, PACK)
-        quantize_w("y", w1_last, 3, 3, PACK)
         gather_e(1)
         product("h", 0, on_scalar, (3, 4))
         product("h", 1, on_scalar, (5, 6))
@@ -274,15 +271,15 @@ def tile_picked_edgeatt_sigmoid_lo_kernel(
         store_messages(2, 4, 512, 768)
         interleave(on_scalar, 512, 768)
         gather_h(2, 768, U)
-        gather_h(3, 896, U)
         gather_h(3, 768, 896)
+        gather_h(3, 896, U)
         store_messages(2, 4, 768, U)
-        interleave(on_scalar, 768, 896)
+        interleave(on_scalar, 896, U)
         quantize_out(0, 512)
         store_words(0, 512)
-        interleave(on_vector, 896, U)
-        quantize_out(512, 768)
-        store_words(512, 768)
-        quantize_out(768, U)
-        store_words(768, U)
+        interleave(on_vector, 768, 896)
+        quantize_out(512, 896)
+        store_words(512, 896)
+        quantize_out(896, U)
+        store_words(896, U)
         store_scales()

@@ -45,7 +45,7 @@ def tile_picked_edgeatt_sigmoid_lo_kernel(
         planes = [keep.tile([P, T], F32, name="plane_%d" % j) for j in range(PACK)]
 
         def load_w(w, label):
-            raw = keep.tile([P, PACK, N], F32, name="w_raw_%s" % label)
+            raw = keep.tile([P, PACK, N], F32, name="w_raw_%s" % label, tag="w_raw_%s" % label, align_bytes=64)
             nc.sync.dma_start(out=raw[:], in_=w.rearrange("(p j) c -> p j c", j=PACK))
             return raw
 
@@ -54,10 +54,10 @@ def tile_picked_edgeatt_sigmoid_lo_kernel(
         for j in range(1, PACK):
             nc.sync.dma_start(out=planes[j][:], in_=x_rows[:, j, :])
         w1_raw = load_w(w1, "y")
-        nc.sync.dma_start(dst_sb[:], dst)
         w2_raw = load_w(w2, "e")
-        nc.sync.dma_start(src_sb[:], src)
+        nc.sync.dma_start(dst_sb[:], dst)
         w3_raw = load_w(w3, "h")
+        nc.sync.dma_start(src_sb[:], src)
 
         picked = [keep.tile([P, 2 * S], BF16, name="picked_%d" % a, tag="picked_%d" % a, align_bytes=64) for a in range(2)]
         x_grouped = keep.tile([P, PACK * S], BF16, name="x_grouped", tag="x_grouped", align_bytes=64)
@@ -100,8 +100,8 @@ def tile_picked_edgeatt_sigmoid_lo_kernel(
             )
             return grouped
 
-        def quantize_w(n, grouped, first, lo, hi):
-            codes = keep.tile([P, (hi - lo) * P], U32, name="w_codes_%s_%d" % (n, lo), align_bytes=64)
+        def quantize_w(n, grouped, first, lo, hi, tag):
+            codes = keep.tile([P, (hi - lo) * P], U32, name="w_codes_%s_%d" % (n, lo), tag=tag, align_bytes=64)
             scales = keep.tile([P, (hi - lo) * P], U8, name="w_scales_%s_%d" % (n, lo), align_bytes=64)
             nc.vector.quantize_mx(
                 out=codes[:].bitcast(FP8X4),
@@ -214,29 +214,28 @@ def tile_picked_edgeatt_sigmoid_lo_kernel(
         place_x(1, 512, 768)
         quantize_x(0, 512, "x_codes_0")
         place_x(1, 768, S)
-        w1_first = cast_w(on_scalar, "y", w1_raw, 0, 1, "w1_first", "p m j t")
+        w1_low = cast_w(on_scalar, "y", w1_raw, 0, 2, "w1_low", "p m j t")
         quantize_x(512, 768, "x_codes_512")
-        quantize_w("y", w1_first, 0, 0, 1)
-        quantize_x(768, S, "w1_first")
-        w1_rest = cast_w(on_scalar, "y", w1_raw, 1, PACK, "w1_rest", "p m j t")
+        quantize_w("y", w1_low, 0, 0, 2, "codes_y0")
+        quantize_x(768, S, "w1_low")
+        w1_high = cast_w(on_scalar, "y", w1_raw, 2, PACK, "w1_high", "p m j t")
         piece("y", 0, 0, 512, on_scalar, 0)
         piece("y", 0, 512, 768, on_scalar, 1)
         piece("y", 0, 768, S, on_scalar, 2)
-        quantize_w("y", w1_rest, 1, 1, PACK)
         gather_y(0)
         w2_grouped = cast_w(on_vector, "e", w2_raw, 0, PACK, "w2_grouped", "p m j t")
         product("y", 1, on_vector, (3, 4))
-        piece("y", 2, 512, S, on_vector, 6)
         gather_y(1)
-        quantize_w("e", w2_grouped, 0, 0, PACK)
+        quantize_w("e", w2_grouped, 0, 0, PACK, "codes_e0")
+        quantize_w("y", w1_high, 2, 2, PACK, "w_raw_e")
         w3_grouped = cast_w(on_vector, "h", w3_raw, 0, PACK, "w3_grouped", "p m j t")
         product("e", 0, on_vector, (7, 0))
         product("e", 1, on_scalar, (1, 2))
-        piece("y", 2, 0, 512, on_vector, 5)
+        product("y", 2, on_vector, (5, 6))
         gather_y(2)
         gather_e(0)
         sigmoid(0)
-        quantize_w("h", w3_grouped, 0, 0, PACK)
+        quantize_w("h", w3_grouped, 0, 0, PACK, "codes_h0")
         gather_e(1)
         product("h", 0, on_scalar, (3, 4))
         product("h", 1, on_scalar, (5, 6))

@@ -89,15 +89,14 @@ def tile_picked_edgeatt_sigmoid_lo_kernel(
         w_codes = {}
         w_scales = {}
 
-        def cast_w(copy, n, raw, lo, hi, tag, walk):
+        def cast_w(shares, n, raw, lo, hi, tag):
             grouped = keep.tile(
                 [P, (hi - lo) * PACK * P], BF16, name="w_grouped_%s_%d" % (n, lo), tag=tag, align_bytes=64
             )
-            dealt = raw[:].rearrange("p j (m t) -> p j m t", t=PACK)[:, :, :, lo:hi]
-            copy(
-                out=grouped[:].rearrange("p (t m j) -> p t m j", m=P, j=PACK).rearrange("p t m j -> " + walk),
-                in_=dealt.rearrange("p j m t -> " + walk),
-            )
+            slots = grouped[:].rearrange("p (t m j) -> p m j t", m=P, j=PACK)
+            dealt = raw[:].rearrange("p j (m t) -> p m j t", t=PACK)[:, :, :, lo:hi]
+            for copy, first, last in shares:
+                copy(out=slots[:, first:last], in_=dealt[:, first:last])
             return grouped
 
         def quantize_w(n, grouped, first, lo, hi, tag):
@@ -112,15 +111,19 @@ def tile_picked_edgeatt_sigmoid_lo_kernel(
                 w_codes[n, t] = codes[:, (t - lo) * P : (t - lo + 1) * P]
                 w_scales[n, t] = scales[:, (t - lo) * P : (t - lo + 1) * P]
 
-        results = {
-            (n, t): keep.tile([P, S + SPARE], F32, name="result_%s_%d" % (n, t)) for n in "yeh" for t in range(PACK)
-        }
+        warm = keep.tile([P, 2], F32, name="warm")
+        nc.gpsimd.memset(warm[:, 0:1], 0.0)
+        nc.scalar.activation(out=warm[:, 1:2], in_=warm[:, 0:1], func=SIGMOID)
+
+        by_halves = (("y", 3), ("e", 3), ("h", 2), ("h", 3))
+        results = {}
         for n in "yeh":
             for t in range(PACK):
-                nc.gpsimd.memset(results[n, t][:, S:], 0.0)
+                spare = 0 if (n, t) in by_halves else SPARE
+                results[n, t] = keep.tile([P, S + spare], F32, name="result_%s_%d" % (n, t))
+                if spare:
+                    nc.gpsimd.memset(results[n, t][:, S:], 0.0)
 
-        warm = keep.tile([P, 1], F32, name="warm")
-        nc.scalar.activation(out=warm[:], in_=results["y", 0][:, S : S + 1], func=SIGMOID)
 
         def piece(n, t, lo, hi, copy, bank):
             acc = psum.tile([P, hi - lo], F32, name="acc_%s_%d_%d" % (n, t, lo), tag="bank_%d" % bank)
@@ -214,21 +217,21 @@ def tile_picked_edgeatt_sigmoid_lo_kernel(
         place_x(1, 512, 768)
         quantize_x(0, 512, "x_codes_0")
         place_x(1, 768, S)
-        w1_low = cast_w(on_scalar, "y", w1_raw, 0, 2, "w1_low", "p m j t")
+        w1_low = cast_w([(on_scalar, 0, P)], "y", w1_raw, 0, 2, "w1_low")
         quantize_x(512, 768, "x_codes_512")
         quantize_w("y", w1_low, 0, 0, 2, "codes_y0")
         quantize_x(768, S, "w1_low")
-        w1_high = cast_w(on_scalar, "y", w1_raw, 2, PACK, "w1_high", "p m j t")
+        w1_high = cast_w([(on_scalar, 0, P)], "y", w1_raw, 2, PACK, "w1_high")
         piece("y", 0, 0, 512, on_scalar, 0)
         piece("y", 0, 512, 768, on_scalar, 1)
         piece("y", 0, 768, S, on_scalar, 2)
         gather_y(0)
-        w2_grouped = cast_w(on_vector, "e", w2_raw, 0, PACK, "w2_grouped", "p m j t")
+        w2_grouped = cast_w([(on_vector, 0, P)], "e", w2_raw, 0, PACK, "w2_grouped")
         product("y", 1, on_vector, (3, 4))
         gather_y(1)
         quantize_w("e", w2_grouped, 0, 0, PACK, "codes_e0")
         quantize_w("y", w1_high, 2, 2, PACK, "w_raw_e")
-        w3_grouped = cast_w(on_vector, "h", w3_raw, 0, PACK, "w3_grouped", "p m j t")
+        w3_grouped = cast_w([(on_vector, 0, P)], "h", w3_raw, 0, PACK, "w3_grouped")
         product("e", 0, on_vector, (7, 0))
         product("e", 1, on_scalar, (1, 2))
         product("y", 2, on_vector, (5, 6))

@@ -34,6 +34,12 @@ def tile_picked_edgeatt_sigmoid_lo_kernel(
         psum = ctx.enter_context(tc.psum_pool(name="psum", bufs=1))
         on_vector, on_scalar = nc.vector.tensor_copy, nc.scalar.copy
 
+        def on_gpsimd(out, in_):
+            nc.gpsimd.tensor_scalar(out=out, in0=in_, scalar1=1.0, scalar2=0.0, op0=MULT, op1=ADD)
+
+        def sbuf(name, cols, dtype, tag=None):
+            return keep.tile([P, cols], dtype, name=name, tag=tag or name, align_bytes=64)
+
         offs_sb = lists.tile([P, S // STRIPE], U16, name="offs_sb")
         src_sb = lists.tile([P, U // STRIPE], U16, name="src_sb")
         dst_sb = lists.tile([P, U // STRIPE], U16, name="dst_sb")
@@ -42,25 +48,24 @@ def tile_picked_edgeatt_sigmoid_lo_kernel(
             return list_sb[:, lo // STRIPE : hi // STRIPE]
 
         x_rows = xT.rearrange("(p j) c -> p j c", j=PACK)
-        planes = [keep.tile([P, T], F32, name="plane_%d" % j) for j in range(PACK)]
+        planes = [sbuf("plane_%d" % j, T, F32) for j in range(PACK)]
+        w_raw = {n: sbuf("w_raw_%s" % n, PACK * N, F32) for n in "yeh"}
 
-        def load_w(w, label):
-            raw = keep.tile([P, PACK, N], F32, name="w_raw_%s" % label, tag="w_raw_%s" % label, align_bytes=64)
-            nc.sync.dma_start(out=raw[:], in_=w.rearrange("(p j) c -> p j c", j=PACK))
-            return raw
+        def load_w(n, w):
+            nc.sync.dma_start(out=w_raw[n][:], in_=w.rearrange("(p j) c -> p (j c)", j=PACK))
 
         nc.sync.dma_start(out=planes[0][:], in_=x_rows[:, 0, :])
         nc.sync.dma_start(offs_sb[:], offs)
         for j in range(1, PACK):
             nc.sync.dma_start(out=planes[j][:], in_=x_rows[:, j, :])
-        w1_raw = load_w(w1, "y")
-        w2_raw = load_w(w2, "e")
+        load_w("y", w1)
+        load_w("e", w2)
         nc.sync.dma_start(dst_sb[:], dst)
-        w3_raw = load_w(w3, "h")
+        load_w("h", w3)
         nc.sync.dma_start(src_sb[:], src)
 
-        picked = [keep.tile([P, 2 * S], BF16, name="picked_%d" % a, tag="picked_%d" % a, align_bytes=64) for a in range(2)]
-        x_grouped = keep.tile([P, PACK * S], BF16, name="x_grouped", tag="x_grouped", align_bytes=64)
+        picked = [sbuf("picked_%d" % a, 2 * S, BF16) for a in range(2)]
+        x_grouped = sbuf("x_grouped", PACK * S, BF16)
         x_codes = {}
         x_scales = {}
 
@@ -77,9 +82,9 @@ def tile_picked_edgeatt_sigmoid_lo_kernel(
             rows = picked[a][:].rearrange("p (j c) -> p c j", j=2)[:, lo:hi, :]
             nc.vector.tensor_copy(out=slots, in_=rows)
 
-        def quantize_x(lo, hi, tag):
-            x_codes[lo] = keep.tile([P, hi - lo], U32, name="x_codes_%d" % lo, tag=tag, align_bytes=64)
-            x_scales[lo] = keep.tile([P, hi - lo], U8, name="x_scales_%d" % lo, align_bytes=64)
+        def quantize_x(lo, hi, tag=None):
+            x_codes[lo] = sbuf("x_codes_%d" % lo, hi - lo, U32, tag)
+            x_scales[lo] = sbuf("x_scales_%d" % lo, hi - lo, U8)
             nc.vector.quantize_mx(
                 out=x_codes[lo][:].bitcast(FP8X4),
                 scales=x_scales[lo][:],
@@ -89,19 +94,19 @@ def tile_picked_edgeatt_sigmoid_lo_kernel(
         w_codes = {}
         w_scales = {}
 
-        def cast_w(shares, n, raw, lo, hi, tag):
-            grouped = keep.tile(
-                [P, (hi - lo) * PACK * P], BF16, name="w_grouped_%s_%d" % (n, lo), tag=tag, align_bytes=64
-            )
-            slots = grouped[:].rearrange("p (t m j) -> p m j t", m=P, j=PACK)
-            dealt = raw[:].rearrange("p j (m t) -> p m j t", t=PACK)[:, :, :, lo:hi]
-            for copy, first, last in shares:
-                copy(out=slots[:, first:last], in_=dealt[:, first:last])
-            return grouped
+        def deal_w(copy, n, grouped, first, lo, hi, m_lo=0, m_hi=P):
+            slots = grouped.rearrange("p (t m j) -> p m j t", m=P, j=PACK)
+            dealt = w_raw[n][:].rearrange("p (j m t) -> p m j t", j=PACK, t=PACK)
+            copy(out=slots[:, m_lo:m_hi, :, lo - first : hi - first], in_=dealt[:, m_lo:m_hi, :, lo:hi])
 
-        def quantize_w(n, grouped, first, lo, hi, tag):
-            codes = keep.tile([P, (hi - lo) * P], U32, name="w_codes_%s_%d" % (n, lo), tag=tag, align_bytes=64)
-            scales = keep.tile([P, (hi - lo) * P], U8, name="w_scales_%s_%d" % (n, lo), align_bytes=64)
+        def deal_w_by_rows(n, grouped):
+            slots = grouped.rearrange("p (t m j) -> p m t j", m=P, j=PACK)
+            dealt = w_raw[n][:].rearrange("p (j m t) -> p m t j", j=PACK, t=PACK)
+            on_gpsimd(out=slots, in_=dealt)
+
+        def quantize_w(n, grouped, first, lo, hi, tag=None):
+            codes = sbuf("w_codes_%s_%d" % (n, lo), (hi - lo) * P, U32, tag)
+            scales = sbuf("w_scales_%s_%d" % (n, lo), (hi - lo) * P, U8)
             nc.vector.quantize_mx(
                 out=codes[:].bitcast(FP8X4),
                 scales=scales[:],
@@ -115,15 +120,14 @@ def tile_picked_edgeatt_sigmoid_lo_kernel(
         nc.gpsimd.memset(warm[:, 0:1], 0.0)
         nc.scalar.activation(out=warm[:, 1:2], in_=warm[:, 0:1], func=SIGMOID)
 
-        by_halves = (("y", 3), ("e", 3), ("h", 2), ("h", 3))
+        by_pieces = (("y", 3), ("e", 3), ("h", 2), ("h", 3))
         results = {}
         for n in "yeh":
             for t in range(PACK):
-                spare = 0 if (n, t) in by_halves else SPARE
+                spare = 0 if (n, t) in by_pieces else SPARE
                 results[n, t] = keep.tile([P, S + spare], F32, name="result_%s_%d" % (n, t))
                 if spare:
                     nc.gpsimd.memset(results[n, t][:, S:], 0.0)
-
 
         def piece(n, t, lo, hi, copy, bank):
             acc = psum.tile([P, hi - lo], F32, name="acc_%s_%d_%d" % (n, t, lo), tag="bank_%d" % bank)
@@ -145,15 +149,20 @@ def tile_picked_edgeatt_sigmoid_lo_kernel(
             for h in range(2):
                 piece(n, t, h * BANK, (h + 1) * BANK, copy, banks[h])
 
-        gate = [keep.tile([P, U], F32, name="gate_%d" % t) for t in range(PACK)]
-        both = [keep.tile([P, U], F32, name="both_%d" % t) for t in range(PACK)]
-        messages = keep.tile([P, PACK * U], F32, name="messages")[:].rearrange("p (t c) -> p t c", t=PACK)
-        out_words = keep.tile([P, U], U32, name="out_words", align_bytes=64)
-        out_scales = keep.tile([P, U], U8, name="out_scales", align_bytes=64)
-        out_grouped = keep.tile([P, PACK * U], BF16, name="out_grouped", align_bytes=64)
+        gate = [sbuf("gate_%d" % t, U, F32) for t in range(PACK)]
+        both = {}
+        messages = sbuf("messages", PACK * U, F32)[:].rearrange("p (t c) -> p t c", t=PACK)
+        out_words = sbuf("out_words", U, U32)
+        out_scales = sbuf("out_scales", U, U8)
+        out_grouped = sbuf("out_grouped", PACK * U, BF16)
         out_rows = out_0.rearrange("(p t) c -> p t c", t=PACK)
         words_hbm = out_1[0].rearrange("p c r -> p (c r)").bitcast(I32)
         scales_hbm = out_2[0].bitcast(I32)
+
+        def sums(first, tag=None):
+            pair = sbuf("both_%d" % first, 2 * U, F32, tag)
+            both[first] = pair[:, :U]
+            both[first + 1] = pair[:, U:]
 
         def gather_y(t, lo=0, hi=U):
             window = results["y", t][:].indirect(entries(dst_sb, lo, hi))
@@ -170,7 +179,7 @@ def tile_picked_edgeatt_sigmoid_lo_kernel(
         def sigmoid(t, lo=0, hi=U):
             nc.scalar.activation(out=gate[t][:, lo:hi], in_=both[t][:, lo:hi], func=SIGMOID)
 
-        def gather_h(t, lo, hi):
+        def gather_h(t, lo=0, hi=U):
             nc.vector.tensor_tensor(
                 out=messages[:, t, lo:hi],
                 in0=results["h", t][:].indirect(entries(src_sb, lo, hi)),
@@ -215,52 +224,58 @@ def tile_picked_edgeatt_sigmoid_lo_kernel(
             gather_x("scalar", 3, lo, hi)
         place_x(1, 0, 512)
         place_x(1, 512, 768)
-        quantize_x(0, 512, "x_codes_0")
+        quantize_x(0, 512)
         place_x(1, 768, S)
-        w1_low = cast_w([(on_scalar, 0, P)], "y", w1_raw, 0, 2, "w1_low")
-        quantize_x(512, 768, "x_codes_512")
-        quantize_w("y", w1_low, 0, 0, 2, "codes_y0")
+        w1_low = sbuf("w1_low", 2 * PACK * P, BF16)[:]
+        deal_w(on_scalar, "y", w1_low, 0, 0, 2)
+        quantize_x(512, 768)
+        quantize_w("y", w1_low, 0, 0, 2)
         quantize_x(768, S, "w1_low")
-        w1_high = cast_w([(on_scalar, 0, P)], "y", w1_raw, 2, PACK, "w1_high")
+        dealt_early = sbuf("dealt_early", 6 * PACK * P, BF16, "dealt")
+        w1_high = dealt_early[:, : 2 * PACK * P]
+        w2_grouped = dealt_early[:, 2 * PACK * P :]
+        deal_w(on_scalar, "y", w1_high, 2, 2, 4)
         piece("y", 0, 0, 512, on_scalar, 0)
         piece("y", 0, 512, 768, on_scalar, 1)
         piece("y", 0, 768, S, on_scalar, 2)
         gather_y(0)
-        w2_grouped = cast_w([(on_vector, 0, P)], "e", w2_raw, 0, PACK, "w2_grouped")
+        deal_w(on_vector, "e", w2_grouped, 0, 0, 4)
+        quantize_w("y", w1_high, 2, 2, 4, "w_raw_e")
+        quantize_w("e", w2_grouped, 0, 0, 4)
+        w3_grouped = sbuf("w3_grouped", PACK * PACK * P, BF16, "dealt")[:]
+        deal_w_by_rows("h", w3_grouped)
         product("y", 1, on_vector, (3, 4))
         gather_y(1)
-        quantize_w("e", w2_grouped, 0, 0, PACK, "codes_e0")
-        quantize_w("y", w1_high, 2, 2, PACK, "w_raw_e")
-        w3_grouped = cast_w([(on_vector, 0, P)], "h", w3_raw, 0, PACK, "w3_grouped")
-        product("e", 0, on_vector, (7, 0))
-        product("e", 1, on_scalar, (1, 2))
-        product("y", 2, on_vector, (5, 6))
-        gather_y(2)
+        product("e", 0, on_vector, (5, 6))
+        product("y", 2, on_vector, (7, 0))
+        product("e", 1, on_vector, (1, 2))
+        quantize_w("h", w3_grouped, 0, 0, 4)
+        sums(0, "w_raw_h")
+        sums(2)
         gather_e(0)
-        sigmoid(0)
-        quantize_w("h", w3_grouped, 0, 0, PACK, "codes_h0")
+        gather_y(2)
         gather_e(1)
+        sigmoid(0)
         product("h", 0, on_scalar, (3, 4))
-        product("h", 1, on_scalar, (5, 6))
-        piece("y", 3, 0, 512, on_vector, 0)
-        gather_h(0, 0, U)
+        gather_h(0)
         store_messages(0, 1, 0, U)
-        product("e", 2, on_scalar, (3, 4))
+        product("e", 2, on_scalar, (5, 6))
         gather_e(2)
+        product("h", 1, on_scalar, (7, 0))
         sigmoid(1)
-        gather_h(1, 0, U)
+        gather_h(1)
         store_messages(1, 2, 0, U)
-        piece("y", 3, 512, S, on_scalar, 5)
-        product("e", 3, on_scalar, (6, 3))
+        product("y", 3, on_scalar, (1, 2))
+        product("e", 3, on_scalar, (3, 4))
         gather_y(3, 0, 512)
         gather_e(3, 0, 512)
         sigmoid(2, 0, 512)
-        product("h", 2, on_scalar, (1, 2))
+        product("h", 2, on_scalar, (5, 6))
         gather_h(2, 0, 512)
         gather_y(3, 512, U)
         gather_e(3, 512, U)
         sigmoid(3, 0, 512)
-        product("h", 3, on_scalar, (4, 5))
+        product("h", 3, on_scalar, (7, 0))
         gather_h(3, 0, 256)
         gather_h(3, 256, 512)
         store_messages(2, 4, 0, 512)

@@ -99,22 +99,19 @@ def tile_picked_edgeatt_sigmoid_lo_kernel(
             dealt = w_raw[n][:].rearrange("p (j m t) -> p m j t", j=PACK, t=PACK)
             copy(out=slots[:, m_lo:m_hi, :, lo - first : hi - first], in_=dealt[:, m_lo:m_hi, :, lo:hi])
 
-        def deal_w_by_rows(n, grouped):
+        def deal_w_by_rows(copy, n, grouped, lo, hi, m_lo=0, m_hi=P):
             slots = grouped.rearrange("p (t m j) -> p m t j", m=P, j=PACK)
             dealt = w_raw[n][:].rearrange("p (j m t) -> p m t j", j=PACK, t=PACK)
-            on_gpsimd(out=slots, in_=dealt)
+            copy(out=slots[:, m_lo:m_hi], in_=dealt[:, m_lo:m_hi, lo:hi])
 
-        def quantize_w(n, grouped, first, lo, hi, tag=None):
-            codes = sbuf("w_codes_%s_%d" % (n, lo), (hi - lo) * P, U32, tag)
-            scales = sbuf("w_scales_%s_%d" % (n, lo), (hi - lo) * P, U8)
-            nc.vector.quantize_mx(
-                out=codes[:].bitcast(FP8X4),
-                scales=scales[:],
-                in_=grouped[:, PACK * P * (lo - first) : PACK * P * (hi - first)],
-            )
-            for t in range(lo, hi):
-                w_codes[n, t] = codes[:, (t - lo) * P : (t - lo + 1) * P]
-                w_scales[n, t] = scales[:, (t - lo) * P : (t - lo + 1) * P]
+        def quantize_w(grouped, row_tiles, tag=None):
+            label = "%s_%d" % row_tiles[0]
+            codes = sbuf("w_codes_" + label, len(row_tiles) * P, U32, tag)
+            scales = sbuf("w_scales_" + label, len(row_tiles) * P, U8)
+            nc.vector.quantize_mx(out=codes[:].bitcast(FP8X4), scales=scales[:], in_=grouped)
+            for i, row_tile in enumerate(row_tiles):
+                w_codes[row_tile] = codes[:, i * P : (i + 1) * P]
+                w_scales[row_tile] = scales[:, i * P : (i + 1) * P]
 
         warm = keep.tile([P, 2], F32, name="warm")
         nc.gpsimd.memset(warm[:, 0:1], 0.0)
@@ -122,12 +119,18 @@ def tile_picked_edgeatt_sigmoid_lo_kernel(
 
         by_pieces = (("y", 3), ("e", 3), ("h", 2), ("h", 3))
         results = {}
+
+        def result(n, t, tag=None):
+            spare = 0 if (n, t) in by_pieces else SPARE
+            results[n, t] = sbuf("result_%s_%d" % (n, t), S + spare, F32, tag)
+            if spare:
+                nc.gpsimd.memset(results[n, t][:, S:], 0.0)
+
+        late_results = ()
         for n in "yeh":
             for t in range(PACK):
-                spare = 0 if (n, t) in by_pieces else SPARE
-                results[n, t] = keep.tile([P, S + spare], F32, name="result_%s_%d" % (n, t))
-                if spare:
-                    nc.gpsimd.memset(results[n, t][:, S:], 0.0)
+                if (n, t) not in late_results:
+                    result(n, t)
 
         def piece(n, t, lo, hi, copy, bank):
             acc = psum.tile([P, hi - lo], F32, name="acc_%s_%d_%d" % (n, t, lo), tag="bank_%d" % bank)
@@ -149,7 +152,7 @@ def tile_picked_edgeatt_sigmoid_lo_kernel(
             for h in range(2):
                 piece(n, t, h * BANK, (h + 1) * BANK, copy, banks[h])
 
-        gate = [sbuf("gate_%d" % t, U, F32) for t in range(PACK)]
+        gate = {}
         both = {}
         messages = sbuf("messages", PACK * U, F32)[:].rearrange("p (t c) -> p t c", t=PACK)
         out_words = sbuf("out_words", U, U32)
@@ -159,10 +162,11 @@ def tile_picked_edgeatt_sigmoid_lo_kernel(
         words_hbm = out_1[0].rearrange("p c r -> p (c r)").bitcast(I32)
         scales_hbm = out_2[0].bitcast(I32)
 
-        def sums(first, tag=None):
-            pair = sbuf("both_%d" % first, 2 * U, F32, tag)
-            both[first] = pair[:, :U]
-            both[first + 1] = pair[:, U:]
+        def gate_tile(t, tag=None):
+            gate[t] = sbuf("gate_%d" % t, U, F32, tag)
+
+        def sum_tile(t, tag=None):
+            both[t] = sbuf("both_%d" % t, U, F32, tag)
 
         def gather_y(t, lo=0, hi=U):
             window = results["y", t][:].indirect(entries(dst_sb, lo, hi))
@@ -229,53 +233,62 @@ def tile_picked_edgeatt_sigmoid_lo_kernel(
         w1_low = sbuf("w1_low", 2 * PACK * P, BF16)[:]
         deal_w(on_scalar, "y", w1_low, 0, 0, 2)
         quantize_x(512, 768)
-        quantize_w("y", w1_low, 0, 0, 2)
+        quantize_w(w1_low, [("y", 0), ("y", 1)])
         quantize_x(768, S, "w1_low")
         dealt_early = sbuf("dealt_early", 6 * PACK * P, BF16, "dealt")
         w1_high = dealt_early[:, : 2 * PACK * P]
-        w2_grouped = dealt_early[:, 2 * PACK * P :]
+        w2_low = dealt_early[:, 2 * PACK * P : 4 * PACK * P]
+        w2_high = dealt_early[:, 4 * PACK * P :]
         deal_w(on_scalar, "y", w1_high, 2, 2, 4)
         piece("y", 0, 0, 512, on_scalar, 0)
         piece("y", 0, 512, 768, on_scalar, 1)
         piece("y", 0, 768, S, on_scalar, 2)
+        gate_tile(0)
         gather_y(0)
-        deal_w(on_vector, "e", w2_grouped, 0, 0, 4)
-        quantize_w("y", w1_high, 2, 2, 4, "w_raw_e")
-        quantize_w("e", w2_grouped, 0, 0, 4)
+        deal_w(on_vector, "e", w2_low, 0, 0, 2)
+        deal_w(on_vector, "e", w2_high, 2, 2, 4)
+        quantize_w(dealt_early[:, : 4 * PACK * P], [("y", 2), ("y", 3), ("e", 0), ("e", 1)])
+        quantize_w(w2_high, [("e", 2), ("e", 3)])
         w3_grouped = sbuf("w3_grouped", PACK * PACK * P, BF16, "dealt")[:]
-        deal_w_by_rows("h", w3_grouped)
-        product("y", 1, on_vector, (3, 4))
+        deal_w_by_rows(on_gpsimd, "h", w3_grouped, 0, 4)
+        piece("y", 1, 0, 512, on_scalar, 3)
+        piece("y", 1, 512, S, on_vector, 4)
+        gate_tile(1)
         gather_y(1)
         product("e", 0, on_vector, (5, 6))
-        product("y", 2, on_vector, (7, 0))
-        product("e", 1, on_vector, (1, 2))
-        quantize_w("h", w3_grouped, 0, 0, 4)
-        sums(0, "w_raw_h")
-        sums(2)
+        product("e", 1, on_vector, (7, 0))
+        product("y", 2, on_vector, (1, 2))
+        piece("y", 3, 0, 512, on_vector, 5)
+        product("e", 2, on_scalar, (3, 4))
+        quantize_w(w3_grouped, [("h", t) for t in range(PACK)])
+        sum_tile(0, "w_raw_h")
+        for t in range(1, PACK):
+            sum_tile(t)
         gather_e(0)
-        gather_y(2)
         gather_e(1)
+        product("h", 0, on_scalar, (6, 7))
+        product("h", 1, on_scalar, (0, 1))
         sigmoid(0)
-        product("h", 0, on_scalar, (3, 4))
         gather_h(0)
         store_messages(0, 1, 0, U)
-        product("e", 2, on_scalar, (5, 6))
-        gather_e(2)
-        product("h", 1, on_scalar, (7, 0))
+        piece("y", 3, 512, S, on_scalar, 0)
         sigmoid(1)
         gather_h(1)
         store_messages(1, 2, 0, U)
-        product("y", 3, on_scalar, (1, 2))
-        product("e", 3, on_scalar, (3, 4))
+        gate_tile(2, "both_1")
+        gather_y(2)
+        product("e", 3, on_scalar, (6, 7))
+        gather_e(2)
+        gate_tile(3, "gate_1")
         gather_y(3, 0, 512)
         gather_e(3, 0, 512)
+        product("h", 2, on_scalar, (6, 7))
         sigmoid(2, 0, 512)
-        product("h", 2, on_scalar, (5, 6))
         gather_h(2, 0, 512)
         gather_y(3, 512, U)
         gather_e(3, 512, U)
+        product("h", 3, on_scalar, (6, 7))
         sigmoid(3, 0, 512)
-        product("h", 3, on_scalar, (7, 0))
         gather_h(3, 0, 256)
         gather_h(3, 256, 512)
         store_messages(2, 4, 0, 512)

@@ -260,34 +260,34 @@ def tile_picked_edgeatt_sigmoid_lo_kernel(
         product("y", 2, on_vector, (1, 2))
         piece("y", 3, 0, 512, on_vector, 5)
         product("e", 2, on_scalar, (3, 4))
+        piece("y", 3, 512, S, on_scalar, 6)
         quantize_w(w3_grouped, [("h", t) for t in range(PACK)])
         sum_tile(0, "w_raw_h")
         for t in range(1, PACK):
             sum_tile(t)
         gather_e(0)
         gather_e(1)
-        product("h", 0, on_scalar, (6, 7))
-        product("h", 1, on_scalar, (0, 1))
+        product("h", 0, on_scalar, (7, 0))
         sigmoid(0)
         gather_h(0)
         store_messages(0, 1, 0, U)
-        piece("y", 3, 512, S, on_scalar, 0)
+        product("h", 1, on_scalar, (1, 2))
         sigmoid(1)
         gather_h(1)
         store_messages(1, 2, 0, U)
         gate_tile(2, "both_1")
         gather_y(2)
-        product("e", 3, on_scalar, (6, 7))
+        product("e", 3, on_scalar, (1, 2))
         gather_e(2)
         gate_tile(3, "gate_1")
         gather_y(3, 0, 512)
         gather_e(3, 0, 512)
-        product("h", 2, on_scalar, (6, 7))
+        product("h", 2, on_scalar, (1, 2))
         sigmoid(2, 0, 512)
         gather_h(2, 0, 512)
         gather_y(3, 512, U)
         gather_e(3, 512, U)
-        product("h", 3, on_scalar, (6, 7))
+        product("h", 3, on_scalar, (1, 2))
         sigmoid(3, 0, 512)
         gather_h(3, 0, 256)
         gather_h(3, 256, 512)

@@ -243,6 +243,7 @@ def tile_picked_edgeatt_sigmoid_lo_kernel(
         piece("y", 0, 0, 512, on_scalar, 0)
         piece("y", 0, 512, 768, on_scalar, 1)
         piece("y", 0, 768, S, on_scalar, 2)
+        piece("y", 1, 0, 512, on_scalar, 3)
         gate_tile(0)
         gather_y(0)
         deal_w(on_vector, "e", w2_low, 0, 0, 2)
@@ -251,7 +252,6 @@ def tile_picked_edgeatt_sigmoid_lo_kernel(
         quantize_w(w2_high, [("e", 2), ("e", 3)])
         w3_grouped = sbuf("w3_grouped", PACK * PACK * P, BF16, "dealt")[:]
         deal_w_by_rows(on_gpsimd, "h", w3_grouped, 0, 4)
-        piece("y", 1, 0, 512, on_scalar, 3)
         piece("y", 1, 512, S, on_vector, 4)
         gate_tile(1)
         gather_y(1)
@@ -268,46 +268,49 @@ def tile_picked_edgeatt_sigmoid_lo_kernel(
         gather_e(0)
         gather_e(1)
         product("h", 0, on_scalar, (7, 0))
+        piece("h", 1, 0, 512, on_scalar, 1)
         sigmoid(0)
         gather_h(0)
         store_messages(0, 1, 0, U)
-        product("h", 1, on_scalar, (1, 2))
+        piece("h", 1, 512, S, on_scalar, 2)
+        piece("e", 3, 0, 512, on_scalar, 1)
         sigmoid(1)
         gather_h(1)
         store_messages(1, 2, 0, U)
-        gate_tile(2, "both_1")
+        gate_tile(2, "w_raw_h")
         gather_y(2)
-        product("e", 3, on_scalar, (1, 2))
+        piece("e", 3, 512, S, on_scalar, 2)
         gather_e(2)
-        gate_tile(3, "gate_1")
+        gate_tile(3, "result_y_2")
         gather_y(3, 0, 512)
+        gather_y(3, 512, U)
         gather_e(3, 0, 512)
+        gather_e(3, 512, U)
         product("h", 2, on_scalar, (1, 2))
         sigmoid(2, 0, 512)
         gather_h(2, 0, 512)
-        gather_y(3, 512, U)
-        gather_e(3, 512, U)
         product("h", 3, on_scalar, (1, 2))
-        sigmoid(3, 0, 512)
-        gather_h(3, 0, 256)
-        gather_h(3, 256, 512)
+        sigmoid(3, 0, 160)
+        gather_h(3, 0, 160)
+        sigmoid(3, 160, 512)
+        gather_h(3, 160, 512)
         store_messages(2, 4, 0, 512)
         sigmoid(2, 512, U)
-        sigmoid(3, 512, U)
-        interleave(on_scalar, 0, 256)
-        interleave(on_scalar, 256, 512)
         gather_h(2, 512, 768)
-        gather_h(3, 512, 768)
-        store_messages(2, 4, 512, 768)
-        interleave(on_scalar, 512, 768)
         gather_h(2, 768, U)
+        store_messages(2, 3, 512, U)
+        sigmoid(3, 512, U)
+        interleave(on_scalar, 0, 160)
+        interleave(on_scalar, 160, 512)
+        gather_h(3, 512, 768)
+        interleave(on_scalar, 512, 768)
         gather_h(3, 768, 896)
         gather_h(3, 896, U)
-        store_messages(2, 4, 768, U)
+        store_messages(3, 4, 512, U)
         interleave(on_scalar, 896, U)
+        interleave(on_vector, 768, 896)
         quantize_out(0, 512)
         store_words(0, 512)
-        interleave(on_vector, 768, 896)
         quantize_out(512, 896)
         store_words(512, 896)
         quantize_out(896, U)

@@ -259,7 +259,9 @@ def tile_picked_edgeatt_sigmoid_lo_kernel(
         product("e", 1, on_vector, (7, 0))
         product("y", 2, on_vector, (1, 2))
         piece("y", 3, 0, 512, on_vector, 5)
-        product("e", 2, on_scalar, (3, 4))
+        piece("e", 2, 768, S, on_vector, 7)
+        piece("e", 2, 0, 512, on_scalar, 3)
+        piece("e", 2, 512, 768, on_scalar, 4)
         piece("y", 3, 512, S, on_scalar, 6)
         quantize_w(w3_grouped, [("h", t) for t in range(PACK)])
         sum_tile(0, "w_raw_h")
@@ -303,12 +305,12 @@ def tile_picked_edgeatt_sigmoid_lo_kernel(
         interleave(on_scalar, 0, 160)
         interleave(on_scalar, 160, 512)
         gather_h(3, 512, 768)
-        interleave(on_scalar, 512, 768)
+        interleave(on_scalar, 512, 704)
         gather_h(3, 768, 896)
         gather_h(3, 896, U)
         store_messages(3, 4, 512, U)
         interleave(on_scalar, 896, U)
-        interleave(on_vector, 768, 896)
+        interleave(on_vector, 704, 896)
         quantize_out(0, 512)
         store_words(0, 512)
         quantize_out(512, 896)

from contextlib import ExitStack

import concourse.mybir as mybir

K, T, S, N, U = 512, 2048, 1024, 512, 1024
FLOPS = 3 * 2 * K * N * S

F32 = mybir.dt.float32
BF16 = mybir.dt.bfloat16
I32 = mybir.dt.int32
U32 = mybir.dt.uint32
U16 = mybir.dt.uint16
U8 = mybir.dt.uint8
FP8X4 = mybir.dt.float8_e4m3fn_x4
ADD = mybir.AluOpType.add
MULT = mybir.AluOpType.mult
COPY = mybir.ActivationFunctionType.Copy
SIGMOID = mybir.ActivationFunctionType.Sigmoid

P = 128
PACK = 4
BANK = 512
STRIPE = 16
SPARE = 16


def tile_picked_edgeatt_sigmoid_lo_kernel(
    tc, xT, w1, w2, w3, offs, src, dst, out_0, out_1, out_2
):
    nc = tc.nc
    with ExitStack() as ctx:
        lists = ctx.enter_context(tc.tile_pool(name="lists", bufs=1))
        keep = ctx.enter_context(tc.tile_pool(name="keep", bufs=1))
        psum = ctx.enter_context(tc.psum_pool(name="psum", bufs=1))
        on_vector, on_scalar = nc.vector.tensor_copy, nc.scalar.copy

        def on_gpsimd(out, in_):
            nc.gpsimd.tensor_scalar(out=out, in0=in_, scalar1=1.0, scalar2=0.0, op0=MULT, op1=ADD)

        def sbuf(name, cols, dtype, tag=None):
            return keep.tile([P, cols], dtype, name=name, tag=tag or name, align_bytes=64)

        offs_sb = lists.tile([P, S // STRIPE], U16, name="offs_sb")
        src_sb = lists.tile([P, U // STRIPE], U16, name="src_sb")
        dst_sb = lists.tile([P, U // STRIPE], U16, name="dst_sb")

        def entries(list_sb, lo, hi):
            return list_sb[:, lo // STRIPE : hi // STRIPE]

        x_rows = xT.rearrange("(p j) c -> p j c", j=PACK)
        planes = [sbuf("plane_%d" % j, T, F32) for j in range(PACK)]
        w_raw = {n: sbuf("w_raw_%s" % n, PACK * N, F32) for n in "yeh"}

        def load_w(n, w):
            nc.sync.dma_start(out=w_raw[n][:], in_=w.rearrange("(p j) c -> p (j c)", j=PACK))

        nc.sync.dma_start(out=planes[0][:], in_=x_rows[:, 0, :])
        nc.sync.dma_start(offs_sb[:], offs)
        for j in range(1, PACK):
            nc.sync.dma_start(out=planes[j][:], in_=x_rows[:, j, :])
        load_w("y", w1)
        load_w("e", w2)
        nc.sync.dma_start(dst_sb[:], dst)
        load_w("h", w3)
        nc.sync.dma_start(src_sb[:], src)

        picked = [sbuf("picked_%d" % a, 2 * S, BF16) for a in range(2)]
        x_grouped = sbuf("x_grouped", PACK * S, BF16)
        x_codes = {}
        x_scales = {}

        def gather_x(engine, j, lo, hi):
            row = picked[j // 2][:, (j % 2) * S + lo : (j % 2) * S + hi]
            window = planes[j][:].indirect(entries(offs_sb, lo, hi))
            if engine == "vector":
                nc.vector.tensor_copy(out=row, in_=window)
            else:
                nc.scalar.activation(out=row, in_=window, func=COPY)

        def place_x(a, lo, hi):
            slots = x_grouped[:].rearrange("p (c a j) -> p c a j", a=2, j=2)[:, lo:hi, a, :]
            rows = picked[a][:].rearrange("p (j c) -> p c j", j=2)[:, lo:hi, :]
            nc.vector.tensor_copy(out=slots, in_=rows)

        def quantize_x(lo, hi, tag=None):
            x_codes[lo] = sbuf("x_codes_%d" % lo, hi - lo, U32, tag)
            x_scales[lo] = sbuf("x_scales_%d" % lo, hi - lo, U8)
            nc.vector.quantize_mx(
                out=x_codes[lo][:].bitcast(FP8X4),
                scales=x_scales[lo][:],
                in_=x_grouped[:, PACK * lo : PACK * hi],
            )

        w_codes = {}
        w_scales = {}

        def deal_w(copy, n, grouped, first, lo, hi, m_lo=0, m_hi=P):
            slots = grouped.rearrange("p (t m j) -> p m j t", m=P, j=PACK)
            dealt = w_raw[n][:].rearrange("p (j m t) -> p m j t", j=PACK, t=PACK)
            copy(out=slots[:, m_lo:m_hi, :, lo - first : hi - first], in_=dealt[:, m_lo:m_hi, :, lo:hi])

        def deal_w_by_rows(copy, n, grouped, lo, hi, m_lo=0, m_hi=P):
            slots = grouped.rearrange("p (t m j) -> p m t j", m=P, j=PACK)
            dealt = w_raw[n][:].rearrange("p (j m t) -> p m t j", j=PACK, t=PACK)
            copy(out=slots[:, m_lo:m_hi], in_=dealt[:, m_lo:m_hi, lo:hi])

        def quantize_w(grouped, row_tiles, tag=None):
            label = "%s_%d" % row_tiles[0]
            codes = sbuf("w_codes_" + label, len(row_tiles) * P, U32, tag)
            scales = sbuf("w_scales_" + label, len(row_tiles) * P, U8)
            nc.vector.quantize_mx(out=codes[:].bitcast(FP8X4), scales=scales[:], in_=grouped)
            for i, row_tile in enumerate(row_tiles):
                w_codes[row_tile] = codes[:, i * P : (i + 1) * P]
                w_scales[row_tile] = scales[:, i * P : (i + 1) * P]

        warm = keep.tile([P, 2], F32, name="warm")
        nc.gpsimd.memset(warm[:, 0:1], 0.0)
        nc.scalar.activation(out=warm[:, 1:2], in_=warm[:, 0:1], func=SIGMOID)

        by_pieces = (("y", 3), ("e", 3), ("h", 2), ("h", 3))
        results = {}

        def result(n, t, tag=None):
            spare = 0 if (n, t) in by_pieces else SPARE
            results[n, t] = sbuf("result_%s_%d" % (n, t), S + spare, F32, tag)
            if spare:
                nc.gpsimd.memset(results[n, t][:, S:], 0.0)

        late_results = ()
        for n in "yeh":
            for t in range(PACK):
                if (n, t) not in late_results:
                    result(n, t)

        def piece(n, t, lo, hi, copy, bank):
            acc = psum.tile([P, hi - lo], F32, name="acc_%s_%d_%d" % (n, t, lo), tag="bank_%d" % bank)
            for first in sorted(x_codes):
                if lo <= first < hi:
                    width = x_codes[first].shape[1]
                    nc.tensor.matmul_mx(
                        out=acc[:, first - lo : first - lo + width],
                        lhsT=w_codes[n, t].bitcast(FP8X4),
                        lhsT_scale=w_scales[n, t],
                        rhs=x_codes[first][:].bitcast(FP8X4),
                        rhs_scale=x_scales[first][:],
                        start=True,
                        stop=True,
                    )
            copy(out=results[n, t][:, lo:hi], in_=acc[:])

        def product(n, t, copy, banks):
            for h in range(2):
                piece(n, t, h * BANK, (h + 1) * BANK, copy, banks[h])

        gate = {}
        both = {}
        messages = sbuf("messages", PACK * U, F32)[:].rearrange("p (t c) -> p t c", t=PACK)
        out_words = sbuf("out_words", U, U32)
        out_scales = sbuf("out_scales", U, U8)
        out_grouped = sbuf("out_grouped", PACK * U, BF16)
        out_rows = out_0.rearrange("(p t) c -> p t c", t=PACK)
        words_hbm = out_1[0].rearrange("p c r -> p (c r)").bitcast(I32)
        scales_hbm = out_2[0].bitcast(I32)

        def gate_tile(t, tag=None):
            gate[t] = sbuf("gate_%d" % t, U, F32, tag)

        def sum_tile(t, tag=None):
            both[t] = sbuf("both_%d" % t, U, F32, tag)

        def gather_y(t, lo=0, hi=U):
            window = results["y", t][:].indirect(entries(dst_sb, lo, hi))
            nc.scalar.activation(out=gate[t][:, lo:hi], in_=window, func=COPY)

        def gather_y_on_vector(t, lo=0, hi=U):
            window = results["y", t][:].indirect(entries(dst_sb, lo, hi))
            nc.vector.tensor_copy(out=gate[t][:, lo:hi], in_=window)

        def gather_e(t, lo=0, hi=U):
            window = results["e", t][:].indirect(entries(src_sb, lo, hi))
            nc.vector.tensor_tensor(out=both[t][:, lo:hi], in0=window, in1=gate[t][:, lo:hi], op=ADD)

        def sigmoid(t, lo=0, hi=U):
            nc.scalar.activation(out=gate[t][:, lo:hi], in_=both[t][:, lo:hi], func=SIGMOID)

        def gather_h(t, lo=0, hi=U):
            nc.vector.tensor_tensor(
                out=messages[:, t, lo:hi],
                in0=results["h", t][:].indirect(entries(src_sb, lo, hi)),
                in1=gate[t][:, lo:hi],
                op=MULT,
            )

        def store_messages(first, last, lo, hi):
            nc.sync.dma_start(out=out_rows[:, first:last, lo:hi], in_=messages[:, first:last, lo:hi])

        def interleave(copy, lo, hi):
            copy(
                out=out_grouped[:, PACK * lo : PACK * hi].rearrange("p (c i t) -> p c t i", i=4, t=PACK),
                in_=messages[:, :, lo:hi].rearrange("p t (c i) -> p c t i", i=4),
            )

        def quantize_out(lo, hi):
            nc.vector.quantize_mx(
                out=out_words[:, lo:hi].bitcast(FP8X4),
                scales=out_scales[:, lo:hi],
                in_=out_grouped[:, PACK * lo : PACK * hi],
            )

        def store_words(lo, hi):
            nc.sync.dma_start(out=words_hbm[:, lo:hi], in_=out_words[:, lo:hi].bitcast(I32))

        def store_scales():
            for q in range(4):
                queue = nc.sync if q % 2 == 0 else nc.scalar
                queue.dma_start(
                    out=scales_hbm[4 * q : 4 * q + 4, :], in_=out_scales[32 * q : 32 * q + 4, :].bitcast(I32)
                )

        for j in range(2):
            gather_x("vector", j, 0, 512)
            gather_x("scalar", j, 512, S)
        place_x(0, 0, S)
        gather_x("scalar", 2, 256, S)
        gather_x("vector", 2, 0, 256)
        gather_x("vector", 3, 0, 256)
        for lo, hi in ((256, 512), (512, 768), (768, S)):
            gather_x("scalar", 3, lo, hi)
        place_x(1, 0, 512)
        place_x(1, 512, 768)
        quantize_x(0, 512)
        place_x(1, 768, S)
        w1_low = sbuf("w1_low", 2 * PACK * P, BF16)[:]
        deal_w(on_scalar, "y", w1_low, 0, 0, 2)
        quantize_x(512, 768)
        quantize_w(w1_low, [("y", 0), ("y", 1)])
        quantize_x(768, S, "w1_low")
        dealt_early = sbuf("dealt_early", 6 * PACK * P, BF16, "dealt")
        w1_high = dealt_early[:, : 2 * PACK * P]
        w2_low = dealt_early[:, 2 * PACK * P : 4 * PACK * P]
        w2_high = dealt_early[:, 4 * PACK * P :]
        deal_w(on_scalar, "y", w1_high, 2, 2, 4)
        piece("y", 0, 0, 512, on_scalar, 0)
        piece("y", 0, 512, 768, on_scalar, 1)
        piece("y", 0, 768, S, on_scalar, 2)
        piece("y", 1, 0, 512, on_scalar, 3)
        gate_tile(0)
        gather_y(0)
        deal_w(on_vector, "e", w2_low, 0, 0, 2)
        deal_w(on_vector, "e", w2_high, 2, 2, 4)
        quantize_w(dealt_early[:, : 4 * PACK * P], [("y", 2), ("y", 3), ("e", 0), ("e", 1)])
        quantize_w(w2_high, [("e", 2), ("e", 3)])
        w3_grouped = sbuf("w3_grouped", PACK * PACK * P, BF16, "dealt")[:]
        deal_w_by_rows(on_gpsimd, "h", w3_grouped, 0, 4)
        piece("y", 1, 512, S, on_vector, 4)
        gate_tile(1)
        gather_y(1)
        product("e", 0, on_vector, (5, 6))
        product("e", 1, on_vector, (7, 0))
        product("y", 2, on_vector, (1, 2))
        piece("y", 3, 0, 512, on_vector, 5)
        piece("e", 2, 768, S, on_vector, 7)
        piece("e", 2, 0, 512, on_scalar, 3)
        piece("e", 2, 512, 768, on_scalar, 4)
        piece("y", 3, 512, S, on_scalar, 6)
        quantize_w(w3_grouped, [("h", t) for t in range(PACK)])
        sum_tile(0, "w_raw_h")
        for t in range(1, PACK):
            sum_tile(t)
        gather_e(0)
        gather_e(1)
        product("h", 0, on_scalar, (7, 0))
        piece("h", 1, 0, 512, on_scalar, 1)
        sigmoid(0)
        gather_h(0)
        store_messages(0, 1, 0, U)
        piece("h", 1, 512, S, on_scalar, 2)
        piece("e", 3, 0, 512, on_scalar, 1)
        sigmoid(1)
        gather_h(1)
        store_messages(1, 2, 0, U)
        gate_tile(2, "w_raw_h")
        gather_y(2)
        piece("e", 3, 512, S, on_scalar, 2)
        gather_e(2)
        gate_tile(3, "result_y_2")
        gather_y(3, 0, 512)
        gather_y(3, 512, U)
        gather_e(3, 0, 512)
        gather_e(3, 512, U)
        product("h", 2, on_scalar, (1, 2))
        sigmoid(2, 0, 512)
        gather_h(2, 0, 512)
        product("h", 3, on_scalar, (1, 2))
        sigmoid(3, 0, 160)
        gather_h(3, 0, 160)
        sigmoid(3, 160, 512)
        gather_h(3, 160, 512)
        store_messages(2, 4, 0, 512)
        sigmoid(2, 512, U)
        gather_h(2, 512, 768)
        gather_h(2, 768, U)
        store_messages(2, 3, 512, U)
        sigmoid(3, 512, U)
        interleave(on_scalar, 0, 160)
        interleave(on_scalar, 160, 512)
        gather_h(3, 512, 768)
        interleave(on_scalar, 512, 704)
        gather_h(3, 768, 896)
        gather_h(3, 896, U)
        store_messages(3, 4, 512, U)
        interleave(on_scalar, 896, U)
        interleave(on_vector, 704, 896)
        quantize_out(0, 512)
        store_words(0, 512)
        quantize_out(512, 896)
        store_words(512, 896)
        quantize_out(896, U)
        store_words(896, U)
        store_scales()
